import numpy as np, ml_dtypes
CORES = [36,164,52,180,100,228,116,244]
N = 8
import mx_ref
BF = ml_dtypes.bfloat16
def cols(t, e):
    v = np.concatenate([t.reshape(128, -1, 4), np.zeros((128, 1, 4), BF)], axis=1)
    return np.ascontiguousarray(v[:, e]).reshape(128, -1)
def cut(t, i, w=512):
    return t[:, w * i:w * i + w]
def f(rng, *shape):
    return mx_ref.flush((rng.standard_normal(shape, dtype=np.float32) * np.exp2(rng.integers(-2, 3, shape[:-1] + (1,)))).astype(BF))
def wide(rng, *shape, cols=0):
    v = rng.standard_normal(shape, dtype=np.float32) * np.exp2(rng.integers(-12, 13, shape)).astype(np.float32)
    if cols: v *= np.repeat(np.exp2(rng.integers(-cols, cols + 1, shape[:-2] + (1, shape[-1] // 4))) * (rng.random(shape[:-2] + (1, shape[-1] // 4)) > 0.0625), 4, axis=-1).astype(np.float32)
    return mx_ref.flush(v.astype(BF))
WD, T, PL, CP, NC = 8, 128, 64, 8, 32
def scores(u, x):
    return np.stack([mx_ref.matmul(mx_ref.quantize(u[r]), mx_ref.quantize(x[r]))[0] for r in range(N)])
def fronts(P):
    a = np.zeros(P.shape, bool)
    v, h = P[1:] != P[:-1], P[:, 1:] != P[:, :-1]
    a[1:] |= v; a[:-1] |= v; a[:, 1:] |= h; a[:, :-1] |= h
    return a
def dealt(P):
    i, j = np.nonzero(fronts(P))
    g = np.full((16 * N + 2, WD + 2), -1)
    g[1:-1, 1:-1] = np.arange(N * T).reshape(16 * N, WD)
    n = np.arange(len(i)); D = np.full((N, PL, 5), -1)
    D[(n // 8) % N, 8 * (n // (8 * N)) + n % 8] = np.stack([g[i + 1, j + 1], g[i, j + 1], g[i + 2, j + 1], g[i + 1, j], g[i + 1, j + 2]], axis=1)
    return D
def needed(P):
    return np.stack([np.bincount(e[e >= 0] // T, minlength=N) for e in [np.unique(k) for k in dealt(P)]])
def broken(P):
    if np.sum(fronts(P)) > PL * N: return ["too many active cells"]
    b = []; D = dealt(P)
    for r in range(N):
        c, e = D[r, :, 0], np.unique(D[r])
        if np.bincount(c[c >= 0] // T, minlength=N).max() > CP: b.append("cells of one stripe dealt to one rank")
        if np.bincount(e[e >= 0] // T, minlength=N).max() > NC: b.append("columns of one stripe that one rank needs")
    return b
def smooth(rng, i):
    a, b = np.indices((16 * N, WD)); g = 0
    for _ in range(6):
        t, k, p = rng.uniform(-1, 1), 0.7 * 0.97 ** i * rng.uniform(0.7, 1.4), rng.uniform(0, 6.2832)
        g = g + np.cos(k * (np.cos(t) * a + np.sin(t) * b) + p)
    return g > 0
def straight(rng, i):
    a = np.indices((16 * N, WD))[0]
    return ((a + rng.integers(1, 4)) // 4) % 2 == 0
def islands(rng, i):
    at = [(0, 0), (15, WD // 2)]
    for c in rng.permutation(N * T):
        if len(at) >= int(N * T * 0.0625 * 0.98 ** i): break
        p, q = divmod(int(c), WD)
        if all(abs(p - a) + abs(q - b) >= 3 for a, b in at): at.append((p, q))
    P = np.zeros((16 * N, WD), bool)
    for p, q in at: P[p, q] = True
    return P
def few(rng, i):
    gone = [int(q) for q in 1 + rng.permutation(N - 1)[:rng.integers(1, 3)]]
    if len(gone) == 2 and abs(gone[0] - gone[1]) == 1: gone.pop()
    here = [q for q in range(N) if q not in gone]
    free = [q for q in here if q - 1 not in gone and q + 1 not in gone]
    P = np.zeros((16 * N, WD), bool)
    for q in here:
        if q - 1 in gone: P[16 * q + 1, rng.integers(0, WD)] = True
        if q + 1 in gone: P[16 * q + 14, rng.integers(0, WD)] = True
    for q in free + here[:rng.integers(0, 2)]: P[16 * q + rng.integers(1, 16 if q + 1 in here else 15), rng.integers(0, WD)] = True
    return P
def heavy(rng, i):
    a, b = np.indices((16 * N, WD)); n = np.zeros(a.shape, int); most = rng.integers(0, N)
    low = b % 2 == 1 if WD == 8 else ((b % 2 == 0) & (b > 0)) | (b == WD - 1)
    for r in range(N):
        if r == most:
            for k in (6, 10): n += a >= 16 * r + k + low
            n += a >= 16 * r + 14
            if WD == 8: n[16 * r + 2, 0] += 1
            else: n += a >= 16 * r + 2
        else:
            w = rng.integers(5, 12) + max(0, 3 - 0.1 * i) * np.sin(rng.uniform(0.2, 0.8) * np.arange(WD) + rng.uniform(0, 6.2832))
            n += a >= 16 * r + np.clip(np.rint(w), 2, 14)[None, :]
    return n % 2 == 0
def borders(rng, i):
    a, b = np.indices((16 * N, WD))
    return (a // 16 + (b < rng.integers(1, WD))) % 2 == 0
def drawn(rng, make, uneven=False, idle=False):
    for i in range(50):
        P = make(rng, i) ^ bool(rng.integers(0, 2))
        c = fronts(P).reshape(N, T).sum(axis=1)
        if c.sum() < (1 if idle else 8 * N) or broken(P): continue
        m = needed(P) * (1 - np.eye(N, dtype=int))
        if uneven and (c.max() < 3 * c.min() or m.max() != NC): continue
        if idle and not 1 <= (c == 0).sum() <= 2: continue
        if idle and (c.sum() > 8 * (N - 1) or (c.sum() - 1) % 8 < 3): continue
        if idle and not (m.sum(axis=0)[c == 0] > 0).all(): continue
        return P
    raise RuntimeError("no field in 50 tries")
def sized(t):
    v = t.astype(np.float32)
    return np.where(np.abs(v) < 2.0 ** -30, np.float32(0), v).astype(BF)
def plant(rng, P, spread=False):
    u = sized(f(rng, 128, 512)); qu = mx_ref.quantize(u)
    x = np.zeros((N, 128, T, 4), BF); want = P.reshape(N, T)
    for r in range(N):
        left = np.arange(T)
        for i in range(50):
            k = len(left); m = 8 * -(-k // 8)
            t = sized(wide(rng, 128, 4 * m, cols=2) if spread else f(rng, 128, 4 * m))
            s = mx_ref.matmul(qu, mx_ref.quantize(t))[0][:k]
            turn = np.where((s > 0) == want[r, left], 1, -1)
            t = (t.astype(np.float32).reshape(128, m, 4)[:, :k] * turn[None, :, None]).astype(BF)
            ok = np.abs(s) > 32
            x[r][:, left[ok]] = t[:, ok]
            left = left[~ok]
            if len(left) == 0: break
        else: raise RuntimeError("scores too small in 50 tries")
    return {"x": x.reshape(N, 128, 4 * T), "u": np.stack([u] * N), "w": sized(f(rng, N, 128, 5120))}
def setup_inputs(rng):
    return plant(rng, drawn(rng, smooth))
def setup_inputs_few(rng):
    return plant(rng, drawn(rng, few, idle=True))
def setup_inputs_near(rng):
    for i in range(50):
        d = plant(rng, drawn(rng, borders))
        s = scores(d["u"], d["x"])
        e = 1 + int(np.floor(np.log2(float(np.abs(s).min()))))
        d["u"] = sized((d["u"].astype(np.float32) * np.float32(2.0 ** -e)).astype(BF))
        t = scores(d["u"], d["x"])
        if 0.5 < np.abs(t).min() <= 1 and np.array_equal(t > 0, s > 0): return d
    raise RuntimeError("no scores near 0.5 in 50 tries")
def setup_inputs_spread(rng):
    return plant(rng, drawn(rng, islands), spread=True)
def setup_inputs_straight(rng):
    return plant(rng, drawn(rng, straight))
def setup_inputs_uneven(rng):
    return plant(rng, drawn(rng, heavy, uneven=True))
def check_inputs(d):
    b = []
    for k in ("x", "u", "w"):
        v = np.abs(d[k].astype(np.float32))
        if not ((v == 0) | ((v >= 2.0 ** -30) & (v <= 2.0 ** 30))).all(): b.append("sizes of " + k)
    if b: return b
    for r in range(N):
        if not np.array_equal(d["u"][r].astype(np.float32), d["u"][0].astype(np.float32)): b.append("u")
    s = scores(d["u"], d["x"])
    if not (np.abs(s) > 0.5).all(): b.append("score")
    return b + broken((s > 0).reshape(16 * N, WD))
def reference(x, u, w):
    P = (scores(u, x) > 0).reshape(16 * N, WD)
    D = dealt(P)
    m = max(8, 8 * -(-int(np.sum(fronts(P))) // (8 * N)))
    X = np.concatenate(list(x), axis=1)
    y = np.zeros((N, 128, 2 * PL), np.float32)
    for r in range(N):
        for k in range(5):
            q = mx_ref.quantize(cols(X, D[r, :m, k]))
            for o in range(2): y[r][:, PL * o:PL * o + m] += mx_ref.matmul(mx_ref.quantize(cut(w[r], 2 * k + o)), q)
    return {"y": y}

@@ -1,0 +1,402 @@
+from concourse.bass import DstId, RemoteDMATransfer
+from concourse.mybir import dt, AluOpType, AxisListType, ActivationFunctionType
+
+A = AluOpType
+F = ActivationFunctionType
+C4, U8 = "float8_e4m3fn_x4", "uint8"
+BF, F32 = "bfloat16", "float32"
+BIG = 1.5 * 2.0 ** 32
+ST = 40
+W0 = 2560
+BATCH = ((0, 1, 2), (4, 5, 6, 7))
+OWN = 3
+SCRATCH = {
+    "xs": ("sbuf", [128, 512], BF), "us": ("sbuf", [128, 4], BF), "ut": ("sbuf", [128, 512], BF),
+    "ln": ("sbuf", [128, 512], BF), "rn": ("sbuf", [128, 512], BF), "zt": ("sbuf", [128, 512], BF),
+    "wt": ("sbuf", [128, 5120], BF),
+    "qu": ("sbuf", [128, 128], C4), "su": ("sbuf", [128, 128], U8),
+    "qx": ("sbuf", [128, 128], C4), "sx": ("sbuf", [128, 128], U8),
+    "wx": ("sbuf", [128, 416], C4), "swx": ("sbuf", [128, 416], U8),
+    "slota": ("sbuf", [128, 144], C4), "sslota": ("sbuf", [128, 144], U8),
+    "slotb": ("sbuf", [128, 192], C4), "sslotb": ("sbuf", [128, 192], U8),
+    "land": ("sbuf", [128, 512], C4), "sland": ("sbuf", [128, 512], U8),
+    "mv": ("sbuf", [128, 448], C4), "smv": ("sbuf", [128, 448], U8),
+    "qw": ("sbuf", [128, 1280], C4), "sw": ("sbuf", [128, 1280], U8),
+    "sgp": ("sbuf", [128, 18, 10], BF), "nb": ("sbuf", [128, 640], BF), "ow": ("sbuf", [128, 640], BF),
+    "a4": ("sbuf", [128, 640], BF), "nnp": ("sbuf", [128, 144], BF),
+    "mo": ("sbuf", [128, ST * 128], BF), "mg": ("sbuf", [128, 8, 40], BF), "jr": ("sbuf", [128, 8], F32),
+    "cr": ("sbuf", [128, 1], F32), "cr2": ("sbuf", [128, 1], F32), "j3": ("sbuf", [128, 128], F32),
+    "base": ("sbuf", [128, 128], BF), "po": ("sbuf", [128, 128], BF),
+    "pa": ("sbuf", [128, 64], BF), "za": ("sbuf", [128, 64], BF), "cA": ("sbuf", [128, 64], F32),
+    "cB": ("sbuf", [128, 64], F32), "pf": ("sbuf", [128, 64], BF), "zf": ("sbuf", [128, 64], BF),
+    "cc": ("sbuf", [128, 8], F32), "cs": ("sbuf", [128, 64], F32), "aq": ("sbuf", [128, 8], F32),
+    "rr": ("sbuf", [128, 128], BF),
+    "pi": ("sbuf", [128, 1], "int32"), "ci": ("sbuf", [128, 3], "int32"), "cf": ("sbuf", [128, 3], F32),
+    "mi": ("sbuf", [128, 32], "int32"), "mj": ("sbuf", [128, 32], "int32"), "i2": ("sbuf", [128, 1], F32),
+    "rs0": ("sbuf", [128, 64], F32), "rs": ("sbuf", [128, 64], F32),
+    "c1": ("sbuf", [128, 1], F32), "mh": ("sbuf", [128, 32], F32),
+    "m1": ("sbuf", [128, 32], F32), "kk": ("sbuf", [128, 2], F32), "hs": ("sbuf", [128, 1], F32),
+    "thr": ("sbuf", [128, 1], F32),
+    "cm": ("sbuf", [128, 128], BF), "acl": ("sbuf", [128, 1], F32), "cn": ("sbuf", [128, 128], BF),
+    "it": ("sbuf", [128, 64], F32), "tt": ("sbuf", [128, 64], F32), "ss": ("sbuf", [128, 64], F32),
+    "off": ("sbuf", [128, 24], "uint16"), "offo": ("sbuf", [128, 4], "uint16"),
+    "n0": ("sbuf", [128, 4], F32), "n2": ("sbuf", [128, 4], F32),
+    "kr0": ("sbuf", [128, 5], F32), "kr": ("sbuf", [128, 5], F32), "cq": ("sbuf", [128, 32], F32),
+    "sq": ("sbuf", [128, 32], F32), "offr": ("sbuf", [128, 20], "uint16"),
+    "yo": ("sbuf", [128, 128], F32),
+    "sc": ("psum", [128, 512], F32), "ps": ("psum", [128, 1024], F32),
+}
+SEMAPHORES = ["v", "z", "du", "dx", "dl", "dw0", "dw1", "gi", "gi2", "gi3", "ect", "eut", "eu", "eq", "pm", "esg", "eow",
+              "s1", "ea", "em", "so", "sz", "ec", "eza", "sk", "sk2", "ecr", "ecr2", "eth", "err", "sa", "et", "eo", "epa",
+              "esa", "epb", "esb", "eo2", "ep2", "es2", "ew", "er", "py0", "py1", "yv", "ys", "dy", "vp", "vq", "va", "vb",
+              "halo", "msg", "cod", "loc", "lm"] + ["kv%d" % k for k in range(5)] + ["ks%d" % k for k in range(5)]
+
+
+def rank_program(g, core, T, topo):
+    r = T.rank_of(core)
+    if r is None:
+        return
+    N = len(T.cores)
+    V, S, Y, P = g.vector, g.scalar, g.sync, g.tensor
+    cnt = {}
+
+    def inc(i, name, k=1):
+        i.then_inc(T.sem[name], k)
+        cnt[name] = cnt.get(name, 0) + k
+
+    def wait(q, name):
+        q.wait_ge(T.sem[name], cnt[name])
+
+    def v(i):
+        inc(i, "v")
+
+    def vw():
+        wait(V, "v")
+
+    def to(d):
+        rid, pnc = topo.addr(T.cores[d], core)
+        return DstId(rid=rid, pnc=pnc)
+
+    def engs(d, s=r):
+        return topo.engines(T.cores[s], T.cores[d])
+
+    def mask(es):
+        return int(sum(1 << e for e in es))
+
+    others = [(r + j) % N for j in range(1, N)]
+
+    def nears(s):
+        return [d for d in (s - 1, s + 1) if 0 <= d < N]
+
+    near = nears(r)
+
+    def deal(s, b, plane):
+        ds = [(s + j - OWN) % N for j in BATCH[b]]
+        es = engs(ds[0], s)
+        n = len(es) // 4
+        w = [1] * 4 if len(ds) == 4 else [2, 1, 1] if plane else [1, 1, 2]
+        out, at = {}, 0
+        for d, k in zip(ds, w):
+            out[d] = es[at:at + n * k]
+            at += n * k
+        return out
+
+    inc(S.dma_start(T.us[:], T.u[:, 0:4]), "du", 16)
+    inc(Y.dma_start(T.xs[:], T.x[:]), "dx", 16)
+    inc(S.dma_start(T.ln[:, 4:512], T.x[:, 0:508]), "dl", 16)
+    inc(Y.dma_start(T.rn[:, 0:508], T.x[:, 4:512]), "dl", 16)
+    inc(Y.dma_start(T.wt[:, 0:W0], T.w[:, 0:W0]), "dw0", 16)
+
+    inc(g.iota(T.pi[:], [[1, 1]], 0, 8), "gi")
+    inc(g.iota(T.mi[:], [[1, 32]], 256, -1), "gi")
+    inc(g.iota(T.rs0[:], [[0, 8], [1, 8]], 0, 0, allow_small_or_imprecise_dtypes=True), "gi")
+    inc(g.iota(T.i2[:], [[0, 1]], 4, 0, allow_small_or_imprecise_dtypes=True), "gi2")
+    inc(V.memset(T.zt[:], 0.0), "z")
+    v(V.memset(T.ow[:], 1.0))
+    v(V.memset(T.sgp[:], 0.0))
+    v(V.memset(T.nnp[:], 0.0))
+    vw()
+    v(V.memset(T.ow[:, 0:640:5], 0.0))
+
+    wait(S, "z")
+    inc(S.activation(T.nb[:, 4:640:5], T.zt[:, 0:128], F.Copy, bias=-1.0), "ect")
+    wait(S, "ect")
+    for a, b, st, k, c in ((9, 39, 5, 6, -0.75), (609, 639, 5, 6, -0.75), (44, 600, 40, 14, -0.75), (79, 600, 40, 14, -0.75),
+                           (4, 40, 35, 2, -0.5), (604, 640, 35, 2, -0.5)):
+        inc(S.activation(T.nb[:, a:b:st], T.zt[:, 0:k], F.Copy, bias=c), "ect")
+
+    wait(S, "du")
+    inc(S.activation(T.ut[:, 3:512:4], T.zt[:, 0:128], F.Identity, bias=T.us[:, 3:4]), "eut")
+    wait(V, "z")
+    wait(V, "du")
+    for t in range(3):
+        v(V.tensor_scalar(T.ut[:, t:512:4], T.zt[:, 0:128], T.us[:, t:t + 1], None, A.add))
+    wait(V, "eut")
+    vw()
+    inc(V.quantize_mx(T.qu[:], T.su[:], T.ut[:]), "eu")
+    wait(V, "dx")
+    inc(V.quantize_mx(T.qx[:], T.sx[:], T.xs[:]), "eq")
+    wait(P, "eu")
+    wait(P, "eq")
+    inc(P.matmul_mx(T.sc[:, 0:128], T.qu[:], T.su[:], T.qx[:], T.sx[:], True, True), "pm")
+
+    def send_halo(plane, ds, sent):
+        tr = []
+        for i, d in enumerate(ds):
+            a, b = (120, 8) if d > r else (0, 144)
+            es = engs(d)
+            n = len(es) // len(ds)
+            if plane:
+                src, dst = T.sx[:, a:a + 8], T.swx[:, b:b + 8]
+            else:
+                src, dst = T.qx[:, a:a + 8].bitcast(dt.uint8), T.wx[:, b:b + 8].bitcast(dt.uint8)
+            tr.append(RemoteDMATransfer(dst_ids=[to(d)], dma_engine_mask=mask(es[n * i:n * i + n]), remote_sem=T.sem.halo,
+                                        src=src, dst=dst))
+        g.remote_dma_fused(tr, local_sem=T.sem[sent])
+
+    wait(g, "eq")
+    send_halo(1, near[:1], "lm")
+    halo = sum(len(engs(r, d)) + len(engs(r, d)) // len(nears(d)) for d in near)
+
+    wait(V, "pm")
+    inc(V.tensor_scalar(T.sgp[:, 1:17, 1:9], T.sc[:, 0:128], -0.5, 0.5, A.max, A.min), "esg")
+    n1 = 120 if 0 < r < N - 1 else 128
+    b0 = ST * (n1 - 1)
+    wait(S, "esg")
+    inc(S.activation(T.ow[:, 4:640:5], T.sgp[:, 1:17, 1:9], F.Copy), "eow")
+    if r > 0:
+        inc(S.activation(T.mo[:, b0:b0 + 8], T.sgp[:, 1, 1:9], F.Copy, scale=4.0), "s1")
+    if r < N - 1:
+        inc(S.activation(T.mo[:, b0 + 25:b0 + 33], T.sgp[:, 16, 1:9], F.Copy, scale=4.0), "s1")
+    wait(S, "dl")
+    for t in range(4):
+        inc(S.activation(T.ln[:, t:512:32], T.zt[:, 0:16], F.Copy), "sz")
+        inc(S.activation(T.rn[:, 28 + t:512:32], T.zt[:, 0:16], F.Copy), "sz")
+    wait(V, "esg")
+    for k, (a, b) in enumerate(((1, 2), (1, 0), (2, 1), (0, 1))):
+        v(V.tensor_scalar(T.nb[:, k:640:5], T.sgp[:, a:a + 16, b:b + 8], 1.0, None, A.mult))
+    wait(V, "ect")
+    wait(V, "eow")
+    vw()
+    inc(V.tensor_tensor_scan(T.a4[:], T.ow[:], T.nb[:], 0.0, A.mult, A.add), "ea")
+    wait(V, "ea")
+    v(V.tensor_scalar(T.nnp[:, 8:136], T.a4[:, 4:640:5], 0.0, -4.0, A.is_ge, A.mult))
+    wait(V, "s1")
+    vw()
+    d0, d1 = (8, 0) if r == 0 else (8, 16)
+    inc(V.tensor_tensor_scan(T.mo[:, 16:b0 + 17:ST], T.nnp[:, d0:d0 + n1], T.nnp[:, d1:d1 + n1], 1024.0,
+                             A.add, A.add), "em")
+    if r > 0:
+        inc(V.tensor_tensor(T.mo[:, b0 + 8:b0 + 16], T.nnp[:, 8:16], T.sgp[:, 1, 1:9], A.mult), "em")
+    if r < N - 1:
+        inc(V.tensor_tensor(T.mo[:, b0 + 17:b0 + 25], T.nnp[:, 128:136], T.sgp[:, 16, 1:9], A.mult), "em")
+    m0, m1 = (16 if r == 0 else 0), (17 if r == N - 1 else 33)
+    wait(g, "em")
+    wait(g, "s1")
+    g.remote_dma_fused([RemoteDMATransfer(dst_ids=[to(d) for d in others], dma_engine_mask=mask(engs(others[0])),
+                                          remote_sem=T.sem.msg, srcs=[T.mo[:, b0 + m0:b0 + m1]],
+                                          dsts=[T.mg[:, r, m0:m1] for d in others])], local_sem=T.sem.lm)
+    send_halo(0, near, "loc")
+    Y.wait_ge(T.sem.lm, 2 * len(engs(others[0])))
+    inc(Y.dma_start(T.wt[:, W0:5120], T.w[:, W0:5120]), "dw1", 16)
+    if near[1:]:
+        send_halo(1, near[1:], "loc")
+    inc(g.iota(T.n0[:], [[1024, 4]], 64 * r, 0, allow_small_or_imprecise_dtypes=True), "gi3")
+    inc(g.iota(T.kr0[:], [[64, 5]], 0, 0, allow_small_or_imprecise_dtypes=True), "gi3")
+    msg = sum(len(engs(r, d)) for d in others)
+    wait(S, "em")
+    wait(S, "s1")
+    inc(S.activation(T.mg[:, r, m0:m1], T.mo[:, b0 + m0:b0 + m1], F.Copy), "so")
+
+    E = 8 * r
+    wait(V, "gi")
+    v(V.tensor_scalar(T.ci[:, 0:1], T.pi[:], 248, None, A.bitwise_and))
+    v(V.tensor_scalar(T.ci[:, 1:2], T.pi[:], 64, None, A.bitwise_and))
+    v(V.tensor_scalar(T.ci[:, 2:3], T.pi[:], 56, None, A.bitwise_and))
+    v(V.tensor_scalar(T.mj[:], T.mi[:], 7, None, A.bitwise_and))
+    v(V.tensor_scalar(T.rs[:], T.rs0[:], 0.5, None, A.is_gt))
+    if r > 0:
+        inc(V.memset(T.za[:, 0:E], 0.0), "eza")
+    inc(V.memset(T.za[:, E + 1:E + 2], -BIG), "eza")
+    inc(V.memset(T.pa[:, E:E + 1], BIG), "eza")
+    vw()
+    inc(V.tensor_copy(T.cf[:], T.ci[:]), "ec")
+    inc(V.tensor_scalar(T.m1[:], T.mj[:], 0.0, None, A.is_equal), "ec")
+    wait(S, "ec")
+    wait(S, "gi2")
+    inc(S.activation(T.c1[:], T.i2[:], F.Identity, bias=T.cf[:, 0:1]), "sk")
+    inc(S.activation(T.kk[:, 0:1], T.cf[:, 1:2], F.Copy, bias=80.0, scale=-0.125), "sk")
+    inc(S.activation(T.kk[:, 1:2], T.cf[:, 1:2], F.Copy, bias=88.0, scale=2.125), "sk")
+    inc(S.activation(T.hs[:], T.cf[:, 1:2], F.Identity, bias=T.cf[:, 2:3], scale=8.0), "sk")
+    inc(S.activation(T.mh[:], T.m1[:], F.Copy, scale=0.5), "sk")
+    wait(S, "sk")
+    sh = 64 * ((r - OWN) % N)
+    inc(S.activation(T.za[:, E:E + 1], T.c1[:], F.Copy, bias=256.0 - sh, scale=-1.0), "sk2")
+    inc(S.activation(T.pa[:, E + 1:E + 2], T.c1[:], F.Copy, bias=float(sh)), "sk2")
+    v(V.tensor_scalar(T.base[:, 8:120], T.nnp[:, 16:128], 2.0, 8.0, A.mult, A.add))
+    v(V.tensor_scalar(T.base[:, 0:8], T.nnp[:, 8:16], 1.0 if r > 0 else 2.0, 8.0, A.mult, A.add))
+    v(V.tensor_scalar(T.base[:, 120:128], T.nnp[:, 128:136], 1.0 if r < N - 1 else 2.0, 8.0, A.mult, A.add))
+    v(V.memset(T.po[:], 0.0))
+    v(V.memset(T.pf[:], 0.0))
+    v(V.memset(T.zf[:], 0.0))
+    if r == 0:
+        v(V.quantize_mx(T.wx[:, 8:136], T.swx[:, 8:136], T.zt[:]))
+        vw()
+    if r == N - 1:
+        v(V.quantize_mx(T.wx[:, 24:152], T.swx[:, 24:152], T.zt[:]))
+        vw()
+    v(V.quantize_mx(T.wx[:, 16:144], T.swx[:, 16:144], T.xs[:]))
+    wait(V, "sz")
+    v(V.quantize_mx(T.wx[:, 160:288], T.swx[:, 160:288], T.ln[:]))
+    v(V.quantize_mx(T.wx[:, 288:416], T.swx[:, 288:416], T.rn[:]))
+    wait(V, "dw0")
+    inc(V.quantize_mx(T.qw[:, 0:384], T.sw[:, 0:384], T.wt[:, 0:1536]), "ew")
+    vw()
+    wait(V, "ec")
+    wait(V, "sk")
+    wait(V, "eza")
+    wait(V, "sk2")
+
+    if r > 0:
+        S.wait_ge(T.sem.msg, msg)
+        inc(S.activation(T.jr[:, 0:r], T.mg[:, 0:r, 16], F.Copy, accum_out=T.cr[:]), "ecr")
+        wait(S, "ecr")
+        inc(S.activation(T.cr2[:], T.cr[:], F.Copy, bias=-256.0), "ecr2")
+    wait(V, "so")
+    V.wait_ge(T.sem.msg, msg)
+    if r > 0:
+        inc(V.tensor_tensor(T.pa[:, 0:E], T.mg[:, 0:r, 17:25], T.mg[:, 1:r + 1, 0:8], A.mult), "vp")
+    if r > 1:
+        inc(V.tensor_tensor(T.za[:, 8:E], T.mg[:, 0:r - 1, 25:33], T.mg[:, 1:r, 8:16], A.mult), "vp")
+    if r > 0:
+        inc(V.tensor_tensor(T.po[:, 0:8], T.mg[:, r, 8:16], T.mg[:, r - 1, 25:33], A.mult), "vq")
+    if r < N - 1:
+        inc(V.tensor_tensor(T.po[:, 120:128], T.mg[:, r, 17:25], T.mg[:, r + 1, 0:8], A.mult), "vq")
+    if r > 0:
+        wait(V, "vp")
+        wait(V, "ecr")
+    inc(V.tensor_tensor_scan(T.cA[:, 0:E + 2], T.za[:, 0:E + 2], T.pa[:, 0:E + 2], T.cr[:] if r > 0 else 0.0,
+                             A.add, A.add), "va")
+    wait(V, "vq")
+    inc(V.tensor_tensor_scan(T.rr[:], T.base[:], T.po[:], 0.0, A.add, A.add), "err")
+    if r > 0:
+        wait(V, "ecr2")
+    inc(V.tensor_tensor_scan(T.cB[:, 0:E + 2], T.za[:, 0:E + 2], T.pa[:, 0:E + 2], T.cr2[:] if r > 0 else -256.0,
+                             A.add, A.add), "vb")
+    wait(V, "va")
+    inc(V.tensor_scalar(T.thr[:], T.cA[:, E + 1:E + 2], T.cA[:, E - 1:E] if r > 0 else 0.0, None, A.subtract), "eth")
+    wait(V, "err")
+    wait(V, "vb")
+    v(V.tensor_scalar(T.cm[:], T.rr[:], T.cB[:, E - 1:E] if r > 0 else -256.0, T.cB[:, E + 1:E + 2], A.add, A.is_le))
+    wait(S, "err")
+    wait(S, "eth")
+    inc(S.activation(T.j3[:], T.rr[:], F.Sign, bias=T.thr[:], scale=-1.0, accum_out=T.acl[:]), "sa")
+    wait(S, "sa")
+    inc(S.activation(T.it[:, 0:32], T.mh[:], F.Copy, scale=T.acl[:]), "et")
+    vw()
+    v(V.tensor_tensor_scan(T.cn[:], T.cm[:], T.zt[:, 0:128], -64.0, A.add, A.add))
+    vw()
+    v(V.tensor_scalar(T.it[:, 32:64], T.m1[:], T.cn[:, 127:128], None, A.mult))
+    wait(V, "et")
+    vw()
+    v(V.transpose(T.tt[:], T.it[:]))
+    vw()
+    v(V.tensor_tensor_scan(T.ss[:], T.rs[:], T.tt[:], 0.0, A.mult, A.add))
+    vw()
+    kk = [T.kk[:, 0:1], T.kk[:, 1:2], 352.0]
+    for k in range(3):
+        inc(V.tensor_scalar(T.off[:, k:24:3], T.ss[:, 7:64:8], 63.0, kk[k], A.min, A.add), "eo")
+    for q in (V, S):
+        q.wait_ge(T.sem.halo, halo)
+        wait(q, "eo")
+    for b, js in enumerate(BATCH):
+        h = "ab"[b]
+        off = T.off[:, 3 * js[0]:3 * js[0] + 3 * len(js)]
+        inc(V.tensor_copy(T["slot" + h][:].bitcast(dt.uint32), T.wx[:].bitcast(dt.uint32).indirect(off)), "ep" + h)
+        inc(S.activation(T["sslot" + h][:], T.swx[:].indirect(off), F.Copy), "es" + h)
+        for plane in (0, 1):
+            wait(g, ("es" if plane else "ep") + h)
+            tr = []
+            for i, (d, es) in enumerate(deal(r, b, plane).items()):
+                i = 48 * i
+                if plane:
+                    src, dst = T["sslot" + h][:, i:i + 40], T.sland[:, 48 * r:48 * r + 40]
+                else:
+                    src = T["slot" + h][:, i:i + 40].bitcast(dt.uint8)
+                    dst = T.land[:, 48 * r:48 * r + 40].bitcast(dt.uint8)
+                tr.append(RemoteDMATransfer(dst_ids=[to(d)], dma_engine_mask=mask(es), remote_sem=T.sem.cod,
+                                            src=src, dst=dst))
+            g.remote_dma_fused(tr, local_sem=T.sem.loc)
+    cod = 0
+    for s in others:
+        for b in range(len(BATCH)):
+            for plane in (0, 1):
+                cod += len(deal(s, b, plane).get(r, []))
+
+    for k in range(3):
+        inc(V.tensor_scalar(T.offo[:, k:k + 1], T.ss[:, 8 * OWN + 7:8 * OWN + 8], 63.0, kk[k], A.min, A.add), "eo2")
+    v(V.tensor_tensor(T.pf[:, 0:56], T.mg[:, 0:N - 1, 17:25], T.mg[:, 1:N, 0:8], A.mult))
+    v(V.tensor_tensor(T.zf[:, 8:64], T.mg[:, 0:N - 1, 25:33], T.mg[:, 1:N, 8:16], A.mult))
+    v(V.tensor_tensor_scan(T.cc[:], T.mg[:, :, 16], T.zt[:, 0:8], 0.0, A.add, A.add))
+    wait(V, "gi3")
+    v(V.tensor_scalar(T.kr[:], T.kr0[:], T.cf[:, 2:3], 0.125, A.add, A.mult))
+    if r > 0:
+        v(V.tensor_scalar(T.n2[:], T.n0[:], T.hs[:], T.cr[:], A.add, A.add))
+    else:
+        v(V.tensor_scalar(T.n2[:], T.n0[:], T.hs[:], None, A.add))
+    vw()
+    v(V.tensor_tensor_scan(T.cs[:], T.zf[:], T.pf[:], T.cr[:] if r > 0 else 0.0, A.add, A.add))
+    wait(V, "eo2")
+    inc(V.tensor_copy(T.land[:, 48 * r:48 * r + 48].bitcast(dt.uint32),
+                      T.wx[:].bitcast(dt.uint32).indirect(T.offo[:, 0:3])), "ep2")
+    wait(S, "eo2")
+    inc(S.activation(T.sland[:, 48 * r:48 * r + 48], T.swx[:].indirect(T.offo[:, 0:3]), F.Copy), "es2")
+    vw()
+    v(V.tensor_tensor(T.aq[:], T.cc[:], T.cs[:, 7:64:8], A.add))
+    v(V.quantize_mx(T.land[:, 384:512], T.sland[:, 384:512], T.zt[:]))
+    v(V.quantize_mx(T.mv[:, 320:448], T.smv[:, 320:448], T.zt[:]))
+    vw()
+    for c in range(4):
+        v(V.tensor_scalar(T.cq[:, 8 * c:8 * c + 8], T.aq[:], T.n2[:, c:c + 1], 48.0, A.is_le, A.mult))
+    vw()
+    v(V.tensor_tensor_scan(T.sq[:], T.rs[:, 0:32], T.cq[:], 0.0, A.mult, A.add))
+    vw()
+    for k in range(5):
+        inc(V.tensor_scalar(T.offr[:, 4 * k:4 * k + 4], T.sq[:, 7:32:8], T.kr[:, k:k + 1], None, A.add), "er")
+
+    wait(V, "dw1")
+    inc(V.quantize_mx(T.qw[:, 384:896], T.sw[:, 384:896], T.wt[:, 1536:3584]), "ew")
+    inc(V.quantize_mx(T.qw[:, 896:1280], T.sw[:, 896:1280], T.wt[:, 3584:5120]), "ew")
+    vw()
+
+    for q in (V, S):
+        wait(q, "er")
+        wait(q, "ep2")
+        wait(q, "es2")
+        q.wait_ge(T.sem.cod, cod)
+    wait(P, "ew")
+    for k in range(5):
+        o16, at = T.offr[:, 4 * k:4 * k + 4], 64 * (4 - k)
+        inc(V.tensor_copy(T.mv[:, at:at + 64].bitcast(dt.uint32),
+                          T.land[:].bitcast(dt.uint32).indirect(o16)), "kv%d" % k)
+        inc(S.activation(T.smv[:, at:at + 64], T.sland[:].indirect(o16), F.Copy), "ks%d" % k)
+    for k in range(5):
+        at = 64 * (4 - k)
+        wait(P, "kv%d" % k)
+        wait(P, "ks%d" % k)
+        for o in (0, 1):
+            w0 = 128 * (2 * k + o)
+            i = P.matmul_mx(T.ps[:, 512 * o:512 * o + 128], T.qw[:, w0:w0 + 128], T.sw[:, w0:w0 + 128],
+                            T.mv[:, at:at + 128], T.smv[:, at:at + 128], k == 0, k == 4)
+            if k == 4:
+                inc(i, "py%d" % o)
+    wait(V, "py0")
+    inc(V.tensor_copy(T.yo[:, 0:64], T.ps[:, 0:64]), "yv")
+    wait(Y, "yv")
+    inc(Y.dma_start(T.y[:, 0:64], T.yo[:, 0:64]), "dy", 16)
+    wait(S, "py1")
+    inc(S.activation(T.yo[:, 64:128], T.ps[:, 512:576], F.Copy), "ys")
+    wait(S, "ys")
+    inc(S.dma_start(T.y[:, 64:128], T.yo[:, 64:128]), "dy", 16)
+    wait(Y, "dy")
+    g.wait_ge(T.sem.loc, (2 * len(BATCH) + len(near)) * len(engs(others[0])))

@@ -7,56 +7,107 @@ C4, U8 = "float8_e4m3fn_x4", "uint8"
 BF, F32 = "bfloat16", "float32"
 BIG = 1.5 * 2.0 ** 32
 ST = 40
-W0 = 2560
+W0 = 3584
+WQ = 896
+NH = 1
 BATCH = ((0, 1, 2), (4, 5, 6, 7))
 OWN = 3
+PICKS = ((0, 0), (1, 2), (3, 4))
+UP, DOWN = 7, 177
 SCRATCH = {
+    "hq": ("sbuf", [128, 16], C4), "hp": ("sbuf", [128, 128], U8),
+    "hslot": ("sbuf", [128, 96], C4), "shslot": ("sbuf", [128, 96], U8),
     "xs": ("sbuf", [128, 512], BF), "us": ("sbuf", [128, 4], BF), "ut": ("sbuf", [128, 512], BF),
-    "ln": ("sbuf", [128, 512], BF), "rn": ("sbuf", [128, 512], BF), "zt": ("sbuf", [128, 512], BF),
+    "xp": ("sbuf", [128, 18, 40], BF), "zt": ("sbuf", [128, 128], BF),
     "wt": ("sbuf", [128, 5120], BF),
     "qu": ("sbuf", [128, 128], C4), "su": ("sbuf", [128, 128], U8),
     "qx": ("sbuf", [128, 128], C4), "sx": ("sbuf", [128, 128], U8),
-    "wx": ("sbuf", [128, 416], C4), "swx": ("sbuf", [128, 416], U8),
-    "slota": ("sbuf", [128, 144], C4), "sslota": ("sbuf", [128, 144], U8),
+    "wx": ("sbuf", [128, 192], C4), "swx": ("sbuf", [128, 192], U8),
+    "slota": ("sbuf", [128, 192], C4), "sslota": ("sbuf", [128, 192], U8),
     "slotb": ("sbuf", [128, 192], C4), "sslotb": ("sbuf", [128, 192], U8),
-    "land": ("sbuf", [128, 512], C4), "sland": ("sbuf", [128, 512], U8),
-    "mv": ("sbuf", [128, 448], C4), "smv": ("sbuf", [128, 448], U8),
+    "land": ("sbuf", [128, 384], C4), "sland": ("sbuf", [128, 384], U8),
+    "mv": ("sbuf", [128, 384], C4), "smv": ("sbuf", [128, 384], U8),
     "qw": ("sbuf", [128, 1280], C4), "sw": ("sbuf", [128, 1280], U8),
     "sgp": ("sbuf", [128, 18, 10], BF), "nb": ("sbuf", [128, 640], BF), "ow": ("sbuf", [128, 640], BF),
     "a4": ("sbuf", [128, 640], BF), "nnp": ("sbuf", [128, 144], BF),
-    "mo": ("sbuf", [128, ST * 128], BF), "mg": ("sbuf", [128, 8, 40], BF), "jr": ("sbuf", [128, 8], F32),
-    "cr": ("sbuf", [128, 1], F32), "cr2": ("sbuf", [128, 1], F32), "j3": ("sbuf", [128, 128], F32),
+    "mo": ("sbuf", [128, ST * 128], BF), "mg": ("sbuf", [128, 8, 40], BF),
     "base": ("sbuf", [128, 128], BF), "po": ("sbuf", [128, 128], BF),
-    "pa": ("sbuf", [128, 64], BF), "za": ("sbuf", [128, 64], BF), "cA": ("sbuf", [128, 64], F32),
-    "cB": ("sbuf", [128, 64], F32), "pf": ("sbuf", [128, 64], BF), "zf": ("sbuf", [128, 64], BF),
-    "cc": ("sbuf", [128, 8], F32), "cs": ("sbuf", [128, 64], F32), "aq": ("sbuf", [128, 8], F32),
-    "rr": ("sbuf", [128, 128], BF),
-    "pi": ("sbuf", [128, 1], "int32"), "ci": ("sbuf", [128, 3], "int32"), "cf": ("sbuf", [128, 3], F32),
-    "mi": ("sbuf", [128, 32], "int32"), "mj": ("sbuf", [128, 32], "int32"), "i2": ("sbuf", [128, 1], F32),
-    "rs0": ("sbuf", [128, 64], F32), "rs": ("sbuf", [128, 64], F32),
-    "c1": ("sbuf", [128, 1], F32), "mh": ("sbuf", [128, 32], F32),
-    "m1": ("sbuf", [128, 32], F32), "kk": ("sbuf", [128, 2], F32), "hs": ("sbuf", [128, 1], F32),
-    "thr": ("sbuf", [128, 1], F32),
-    "cm": ("sbuf", [128, 128], BF), "acl": ("sbuf", [128, 1], F32), "cn": ("sbuf", [128, 128], BF),
-    "it": ("sbuf", [128, 64], F32), "tt": ("sbuf", [128, 64], F32), "ss": ("sbuf", [128, 64], F32),
-    "off": ("sbuf", [128, 24], "uint16"), "offo": ("sbuf", [128, 4], "uint16"),
-    "n0": ("sbuf", [128, 4], F32), "n2": ("sbuf", [128, 4], F32),
-    "kr0": ("sbuf", [128, 5], F32), "kr": ("sbuf", [128, 5], F32), "cq": ("sbuf", [128, 32], F32),
-    "sq": ("sbuf", [128, 32], F32), "offr": ("sbuf", [128, 20], "uint16"),
+    "pa": ("sbuf", [128, 64], BF), "za": ("sbuf", [128, 64], BF), "cr": ("sbuf", [128, 2], F32),
+    "pp": ("sbuf", [128, 128], BF), "cx": ("sbuf", [128, 128], BF), "cs": ("sbuf", [128, 128], F32),
+    "cA": ("sbuf", [128, 64], F32), "cB": ("sbuf", [128, 64], F32), "rr": ("sbuf", [128, 128], BF),
+    "pi": ("sbuf", [128, 3], "int32"), "ci": ("sbuf", [128, 3], "int32"), "cf": ("sbuf", [128, 3], F32),
+    "jj": ("sbuf", [128, 32], F32), "c0": ("sbuf", [128, 32], F32), "ct": ("sbuf", [128, 32], F32),
+    "posn": ("sbuf", [128, 162], BF), "k1": ("sbuf", [128, 8], F32), "kk": ("sbuf", [128, 3], F32),
+    "cm": ("sbuf", [128, 2, 160], BF), "cn": ("sbuf", [128, 2, 160], BF), "j0": ("sbuf", [128, 8], F32),
+    "tt": ("sbuf", [128, 64], BF), "ss": ("sbuf", [128, 64], F32),
+    "offa": ("sbuf", [128, 12], "uint16"), "offb": ("sbuf", [128, 12], "uint16"), "offo": ("sbuf", [128, 4], "uint16"),
+    "n2": ("sbuf", [128, 4], F32), "jr": ("sbuf", [128, 32], F32), "sq": ("sbuf", [128, 4], F32),
+    "s2": ("sbuf", [128, 4], F32), "of": ("sbuf", [128, 20], F32), "offr": ("sbuf", [128, 20], "uint16"),
+    "nn": ("sbuf", [128, 64], F32), "mj": ("sbuf", [128, 64], F32), "mk": ("sbuf", [128, 64], F32),
+    "jk": ("sbuf", [128, 800], BF), "jl": ("sbuf", [128, 384], BF),
     "yo": ("sbuf", [128, 128], F32),
     "sc": ("psum", [128, 512], F32), "ps": ("psum", [128, 1024], F32),
 }
-SEMAPHORES = ["v", "z", "du", "dx", "dl", "dw0", "dw1", "gi", "gi2", "gi3", "ect", "eut", "eu", "eq", "pm", "esg", "eow",
-              "s1", "ea", "em", "so", "sz", "ec", "eza", "sk", "sk2", "ecr", "ecr2", "eth", "err", "sa", "et", "eo", "epa",
-              "esa", "epb", "esb", "eo2", "ep2", "es2", "ew", "er", "py0", "py1", "yv", "ys", "dy", "vp", "vq", "va", "vb",
-              "halo", "msg", "cod", "loc", "lm"] + ["kv%d" % k for k in range(5)] + ["ks%d" % k for k in range(5)]
+SEMAPHORES = ["v", "msg2", "eoo", "z", "du", "dx", "dw0", "dw1", "dp", "gi", "gi2", "gi3", "gi4", "ect", "eut", "eu", "eq", "pm", "esg",
+              "eow", "s1", "ea", "em", "so", "sx", "ei", "ec", "ec0", "ez", "sk", "s", "ecr", "ecr2", "ecx", "err", "eoa",
+              "eob", "epa", "esa", "epb", "esb", "ep2", "es2", "ew", "er", "er0", "emk", "py0", "py1", "y0", "y1", "dy",
+              "vp", "vq", "va", "vb", "vf", "halo", "msg", "cod", "loc", "lm", "hh", "h0", "h1"
+              ] + ["kv%d" % k for k in range(5)] + ["ks%d" % k for k in range(5)]
+
+
+def mask(es):
+    return int(sum(1 << e for e in es))
+
+
+def helpers(c, topo):
+    return [h for h in topo.cores_of(c) if topo.die(h) == topo.die(c) and h != c][:NH]
+
+
+def hand_on(g, core, s, i, T, topo):
+    N = len(T.cores)
+    near = [d for d in (s - 1, s + 1) if 0 <= d < N]
+    on = topo.engines(T.cores[s], core)
+    off = topo.engines(T.cores[s], T.cores[near[0]])
+
+    def send(items, sem):
+        tr = []
+        for j, (d, src, dst) in enumerate(items):
+            es = topo.engines(core, T.cores[d])
+            n = len(es) // len(items)
+            rid, pnc = topo.addr(T.cores[d], core)
+            tr.append(RemoteDMATransfer(dst_ids=[DstId(rid=rid, pnc=pnc)], dma_engine_mask=mask(es[n * j:n * j + n]),
+                                        remote_sem=sem, src=src, dst=dst))
+        g.remote_dma_fused(tr, local_sem=T.sem.loc)
+
+    g.wait_ge(T.sem.hh, len(on) - len(off))
+    items = []
+    for d in near:
+        b, c = (UP, 8) if d > s else (DOWN, 0)
+        items.append((d, T.hq[:, c:c + 8].bitcast(dt.uint8), T.wx[:, b:b + 8].bitcast(dt.uint8)))
+    send(items, T.sem.halo)
+    d = (s + BATCH[0][0] - OWN) % N
+    g.wait_ge(T.sem.h0, len(on) - len(off))
+    send([(d, T.hslot[:, 0:40].bitcast(dt.uint8), T.land[:, 48 * s:48 * s + 40].bitcast(dt.uint8))], T.sem.cod)
+    g.wait_ge(T.sem.h1, len(on) - len(off))
+    send([(d, T.shslot[:, 0:40], T.sland[:, 48 * s:48 * s + 40])], T.sem.cod)
+    g.wait_ge(T.sem.loc, 3 * len(topo.engines(core, T.cores[near[0]])))
 
 
 def rank_program(g, core, T, topo):
     r = T.rank_of(core)
     if r is None:
+        for s, c in enumerate(T.cores):
+            if core in helpers(c, topo):
+                hand_on(g, core, s, helpers(c, topo).index(core), T, topo)
         return
     N = len(T.cores)
+    hs = helpers(core, topo)
+    on = topo.engines(core, hs[0]) if NH else []
+
+    def toh(i):
+        rid, pnc = topo.addr(hs[i], core)
+        return DstId(rid=rid, pnc=pnc)
+
     V, S, Y, P = g.vector, g.scalar, g.sync, g.tensor
     cnt = {}
 
@@ -73,6 +124,12 @@ def rank_program(g, core, T, topo):
     def vw():
         wait(V, "v")
 
+    def act(out, in_, name, func=F.Copy, **kw):
+        inc(S.activation(out, in_, func, **kw), name)
+
+    def iota(out, pattern, base, name):
+        inc(g.iota(out, pattern, base, 0, allow_small_or_imprecise_dtypes=True), name)
+
     def to(d):
         rid, pnc = topo.addr(T.cores[d], core)
         return DstId(rid=rid, pnc=pnc)
@@ -80,21 +137,26 @@ def rank_program(g, core, T, topo):
     def engs(d, s=r):
         return topo.engines(T.cores[s], T.cores[d])
 
-    def mask(es):
-        return int(sum(1 << e for e in es))
-
     others = [(r + j) % N for j in range(1, N)]
 
     def nears(s):
         return [d for d in (s - 1, s + 1) if 0 <= d < N]
 
     near = nears(r)
+    ne = len(engs(near[0]))
+    sent = {"loc": 0, "lm": 0}
+
+    def remote(tr, es, sem):
+        g.remote_dma_fused(tr, local_sem=T.sem[sem])
+        sent[sem] += es
 
     def deal(s, b, plane):
         ds = [(s + j - OWN) % N for j in BATCH[b]]
         es = engs(ds[0], s)
         n = len(es) // 4
         w = [1] * 4 if len(ds) == 4 else [2, 1, 1] if plane else [1, 1, 2]
+        if b == 0 and NH:
+            return {ds[0]: [e for e in on if e not in es], ds[1]: es[:2 * n], ds[2]: es[2 * n:]}
         out, at = {}, 0
         for d, k in zip(ds, w):
             out[d] = es[at:at + n * k]
@@ -103,34 +165,39 @@ def rank_program(g, core, T, topo):
 
     inc(S.dma_start(T.us[:], T.u[:, 0:4]), "du", 16)
     inc(Y.dma_start(T.xs[:], T.x[:]), "dx", 16)
-    inc(S.dma_start(T.ln[:, 4:512], T.x[:, 0:508]), "dl", 16)
-    inc(Y.dma_start(T.rn[:, 0:508], T.x[:, 4:512]), "dl", 16)
     inc(Y.dma_start(T.wt[:, 0:W0], T.w[:, 0:W0]), "dw0", 16)
 
-    inc(g.iota(T.pi[:], [[1, 1]], 0, 8), "gi")
-    inc(g.iota(T.mi[:], [[1, 32]], 256, -1), "gi")
-    inc(g.iota(T.rs0[:], [[0, 8], [1, 8]], 0, 0, allow_small_or_imprecise_dtypes=True), "gi")
-    inc(g.iota(T.i2[:], [[0, 1]], 4, 0, allow_small_or_imprecise_dtypes=True), "gi2")
+    for c, k in enumerate((8, 32, 16)):
+        inc(g.iota(T.pi[:, c:c + 1], [[1, 1]], 0, k), "gi")
+    iota(T.jj[:], [[0, 4], [32, 8]], 0, "gi2")
+    iota(T.posn[:, 0:128], [[-10, 16], [-1, 8]], 157, "gi3")
     inc(V.memset(T.zt[:], 0.0), "z")
-    v(V.memset(T.ow[:], 1.0))
     v(V.memset(T.sgp[:], 0.0))
+    for k in range(4):
+        v(V.memset(T.ow[:, k:640:5], 1.0 if k else 0.0))
     v(V.memset(T.nnp[:], 0.0))
-    vw()
-    v(V.memset(T.ow[:, 0:640:5], 0.0))
+    v(V.memset(T.xp[:, :, 0:4], 0.0))
+    v(V.memset(T.xp[:, :, 36:40], 0.0))
+    x0, x1 = (0 if r == 0 else 1), (18 if r == N - 1 else 17)
+    if r in (0, N - 1):
+        v(V.memset(T.xp[:, 0 if r == 0 else 17, 4:36], 0.0))
+    wait(V, "gi")
+    inc(V.tensor_scalar(T.ci[:], T.pi[:], 248, None, A.bitwise_and), "ei")
+    I8, S32, P16 = T.cf[:, 0:1], T.cf[:, 1:2], T.cf[:, 2:3]
 
     wait(S, "z")
-    inc(S.activation(T.nb[:, 4:640:5], T.zt[:, 0:128], F.Copy, bias=-1.0), "ect")
+    act(T.nb[:, 4:640:5], T.zt[:], "ect", bias=-1.0)
     wait(S, "ect")
     for a, b, st, k, c in ((9, 39, 5, 6, -0.75), (609, 639, 5, 6, -0.75), (44, 600, 40, 14, -0.75), (79, 600, 40, 14, -0.75),
                            (4, 40, 35, 2, -0.5), (604, 640, 35, 2, -0.5)):
-        inc(S.activation(T.nb[:, a:b:st], T.zt[:, 0:k], F.Copy, bias=c), "ect")
+        act(T.nb[:, a:b:st], T.zt[:, 0:k], "ect", bias=c)
 
     wait(S, "du")
-    inc(S.activation(T.ut[:, 3:512:4], T.zt[:, 0:128], F.Identity, bias=T.us[:, 3:4]), "eut")
+    act(T.ut[:, 3:512:4], T.zt[:], "eut", F.Identity, bias=T.us[:, 3:4])
     wait(V, "z")
     wait(V, "du")
     for t in range(3):
-        v(V.tensor_scalar(T.ut[:, t:512:4], T.zt[:, 0:128], T.us[:, t:t + 1], None, A.add))
+        v(V.tensor_scalar(T.ut[:, t:512:4], T.zt[:], T.us[:, t:t + 1], None, A.add))
     wait(V, "eut")
     vw()
     inc(V.quantize_mx(T.qu[:], T.su[:], T.ut[:]), "eu")
@@ -139,11 +206,16 @@ def rank_program(g, core, T, topo):
     wait(P, "eu")
     wait(P, "eq")
     inc(P.matmul_mx(T.sc[:, 0:128], T.qu[:], T.su[:], T.qx[:], T.sx[:], True, True), "pm")
+    E = 8 * r
+    act(T.pa[:, E:E + 1], T.zt[:, 0:1], "sk", bias=BIG)
+    act(T.za[:, E + 1:E + 2], T.zt[:, 0:1], "sk", bias=-BIG)
+    wait(S, "dx")
+    act(T.xp[:, 1:17, 4:36], T.xs[:], "sx")
 
-    def send_halo(plane, ds, sent):
+    def send_halo(plane, ds, sem):
         tr = []
         for i, d in enumerate(ds):
-            a, b = (120, 8) if d > r else (0, 144)
+            a, b = (120, UP) if d > r else (0, DOWN)
             es = engs(d)
             n = len(es) // len(ds)
             if plane:
@@ -152,26 +224,38 @@ def rank_program(g, core, T, topo):
                 src, dst = T.qx[:, a:a + 8].bitcast(dt.uint8), T.wx[:, b:b + 8].bitcast(dt.uint8)
             tr.append(RemoteDMATransfer(dst_ids=[to(d)], dma_engine_mask=mask(es[n * i:n * i + n]), remote_sem=T.sem.halo,
                                         src=src, dst=dst))
-        g.remote_dma_fused(tr, local_sem=T.sem[sent])
+        remote(tr, ne, sem)
+
+    def feed_halo():
+        es = [e for e in on if e not in engs(near[0])]
+        n = len(es) // len(near)
+        tr = []
+        for i, d in enumerate(near):
+            a, c = (120, 8) if d > r else (0, 0)
+            tr.append(RemoteDMATransfer(dst_ids=[toh(0)], dma_engine_mask=mask(es[n * i:n * i + n]), remote_sem=T.sem.hh,
+                                        src=T.qx[:, a:a + 8].bitcast(dt.uint8), dst=T.hq[:, c:c + 8].bitcast(dt.uint8)))
+        remote(tr, len(es), "loc")
 
     wait(g, "eq")
     send_halo(1, near[:1], "lm")
-    halo = sum(len(engs(r, d)) + len(engs(r, d)) // len(nears(d)) for d in near)
+    halo = sum(ne + ne // len(nears(d)) for d in near)
+
+    n1 = 120 if 0 < r < N - 1 else 128
+    b0 = ST * (n1 - 1)
+    m0, m1 = (16 if r == 0 else 0), (17 if r == N - 1 else 33)
+    out = T.mo[:, b0 + m0:b0 + m1]
+
+    wait(V, "ei")
+    inc(V.tensor_copy(T.cf[:], T.ci[:]), "ec")
 
     wait(V, "pm")
     inc(V.tensor_scalar(T.sgp[:, 1:17, 1:9], T.sc[:, 0:128], -0.5, 0.5, A.max, A.min), "esg")
-    n1 = 120 if 0 < r < N - 1 else 128
-    b0 = ST * (n1 - 1)
     wait(S, "esg")
-    inc(S.activation(T.ow[:, 4:640:5], T.sgp[:, 1:17, 1:9], F.Copy), "eow")
+    act(T.ow[:, 4:640:5], T.sgp[:, 1:17, 1:9], "eow")
     if r > 0:
-        inc(S.activation(T.mo[:, b0:b0 + 8], T.sgp[:, 1, 1:9], F.Copy, scale=4.0), "s1")
+        act(T.mo[:, b0:b0 + 8], T.sgp[:, 1, 1:9], "s1", scale=4.0)
     if r < N - 1:
-        inc(S.activation(T.mo[:, b0 + 25:b0 + 33], T.sgp[:, 16, 1:9], F.Copy, scale=4.0), "s1")
-    wait(S, "dl")
-    for t in range(4):
-        inc(S.activation(T.ln[:, t:512:32], T.zt[:, 0:16], F.Copy), "sz")
-        inc(S.activation(T.rn[:, 28 + t:512:32], T.zt[:, 0:16], F.Copy), "sz")
+        act(T.mo[:, b0 + 25:b0 + 33], T.sgp[:, 16, 1:9], "s1", scale=4.0)
     wait(V, "esg")
     for k, (a, b) in enumerate(((1, 2), (1, 0), (2, 1), (0, 1))):
         v(V.tensor_scalar(T.nb[:, k:640:5], T.sgp[:, a:a + 16, b:b + 8], 1.0, None, A.mult))
@@ -190,78 +274,75 @@ def rank_program(g, core, T, topo):
         inc(V.tensor_tensor(T.mo[:, b0 + 8:b0 + 16], T.nnp[:, 8:16], T.sgp[:, 1, 1:9], A.mult), "em")
     if r < N - 1:
         inc(V.tensor_tensor(T.mo[:, b0 + 17:b0 + 25], T.nnp[:, 128:136], T.sgp[:, 16, 1:9], A.mult), "em")
-    m0, m1 = (16 if r == 0 else 0), (17 if r == N - 1 else 33)
     wait(g, "em")
     wait(g, "s1")
-    g.remote_dma_fused([RemoteDMATransfer(dst_ids=[to(d) for d in others], dma_engine_mask=mask(engs(others[0])),
-                                          remote_sem=T.sem.msg, srcs=[T.mo[:, b0 + m0:b0 + m1]],
-                                          dsts=[T.mg[:, r, m0:m1] for d in others])], local_sem=T.sem.lm)
-    send_halo(0, near, "loc")
-    Y.wait_ge(T.sem.lm, 2 * len(engs(others[0])))
+    for ds, sem in ((others, "msg"),):
+        if ds:
+            remote([RemoteDMATransfer(dst_ids=[to(d) for d in ds], dma_engine_mask=mask(engs(ds[0])),
+                                      remote_sem=T.sem[sem], srcs=[out], dsts=[T.mg[:, r, m0:m1] for d in ds])], ne, "lm")
+    wait(V, "gi2")
+    wait(V, "ec")
+    inc(V.tensor_scalar(T.c0[:], T.jj[:], S32, 8448.0, A.not_equal, A.mult), "ec0")
+    v(V.memset(T.cm[:, :, 128:160], 1.0))
+    v(V.memset(T.posn[:, 128:162], 0.0))
+    if NH:
+        feed_halo()
+    else:
+        send_halo(0, near, "loc")
+    Y.wait_ge(T.sem.lm, sent["lm"])
     inc(Y.dma_start(T.wt[:, W0:5120], T.w[:, W0:5120]), "dw1", 16)
+    inc(Y.dma_start(T.mv[:, 320:384].bitcast(dt.uint8), T.qx[:, 0:64].bitcast(dt.uint8)), "dp", 16)
+    inc(Y.dma_start(T.smv[:, 320:384], T.sx[:, 0:64]), "dp", 16)
     if near[1:]:
         send_halo(1, near[1:], "loc")
-    inc(g.iota(T.n0[:], [[1024, 4]], 64 * r, 0, allow_small_or_imprecise_dtypes=True), "gi3")
-    inc(g.iota(T.kr0[:], [[64, 5]], 0, 0, allow_small_or_imprecise_dtypes=True), "gi3")
-    msg = sum(len(engs(r, d)) for d in others)
+    iota(T.nn[:], [[512, 8], [8, 8]], 64 * r + 4, "gi4")
+    msg = ne * len(others)
+    msg2 = ne * len(others) - msg
+
+    sh = 64 * ((r - OWN) % N)
+    wait(S, "ec")
+    act(T.k1[:, 0:1], P16, "s", bias=1966.0, scale=-10.0 / 128)
+    act(T.k1[:, 1:2], P16, "s", bias=1976.0, scale=-11.0 / 128)
+    act(T.kk[:, 2:3], S32, "sk", bias=1967.0, scale=-8.0)
+    act(T.za[:, E:E + 1], I8, "sk", bias=252.0 - sh, scale=-1.0)
+    act(T.pa[:, E + 1:E + 2], I8, "sk", bias=4.0 + sh)
+    wait(S, "s")
+    act(T.kk[:, 0:1], S32, "sk", F.Identity, bias=T.k1[:, 0:1], scale=-8.0 + 10.0 / 256)
+    act(T.kk[:, 1:2], S32, "sk", F.Identity, bias=T.k1[:, 1:2], scale=-8.0 + 11.0 / 256)
     wait(S, "em")
     wait(S, "s1")
-    inc(S.activation(T.mg[:, r, m0:m1], T.mo[:, b0 + m0:b0 + m1], F.Copy), "so")
-
-    E = 8 * r
-    wait(V, "gi")
-    v(V.tensor_scalar(T.ci[:, 0:1], T.pi[:], 248, None, A.bitwise_and))
-    v(V.tensor_scalar(T.ci[:, 1:2], T.pi[:], 64, None, A.bitwise_and))
-    v(V.tensor_scalar(T.ci[:, 2:3], T.pi[:], 56, None, A.bitwise_and))
-    v(V.tensor_scalar(T.mj[:], T.mi[:], 7, None, A.bitwise_and))
-    v(V.tensor_scalar(T.rs[:], T.rs0[:], 0.5, None, A.is_gt))
+    act(T.mg[:, r, m0:m1], out, "so")
+    wait(S, "ec0")
+    act(T.ct[:], T.c0[:], "sk", bias=-8192.0)
+    lo, hi = (8 if r > 0 else 0), (120 if r < N - 1 else 128)
+    act(T.base[:, lo:hi], T.nnp[:, lo + 8:hi + 8], "sk", bias=8.0, scale=2.0)
     if r > 0:
-        inc(V.memset(T.za[:, 0:E], 0.0), "eza")
-    inc(V.memset(T.za[:, E + 1:E + 2], -BIG), "eza")
-    inc(V.memset(T.pa[:, E:E + 1], BIG), "eza")
-    vw()
-    inc(V.tensor_copy(T.cf[:], T.ci[:]), "ec")
-    inc(V.tensor_scalar(T.m1[:], T.mj[:], 0.0, None, A.is_equal), "ec")
-    wait(S, "ec")
-    wait(S, "gi2")
-    inc(S.activation(T.c1[:], T.i2[:], F.Identity, bias=T.cf[:, 0:1]), "sk")
-    inc(S.activation(T.kk[:, 0:1], T.cf[:, 1:2], F.Copy, bias=80.0, scale=-0.125), "sk")
-    inc(S.activation(T.kk[:, 1:2], T.cf[:, 1:2], F.Copy, bias=88.0, scale=2.125), "sk")
-    inc(S.activation(T.hs[:], T.cf[:, 1:2], F.Identity, bias=T.cf[:, 2:3], scale=8.0), "sk")
-    inc(S.activation(T.mh[:], T.m1[:], F.Copy, scale=0.5), "sk")
-    wait(S, "sk")
-    sh = 64 * ((r - OWN) % N)
-    inc(S.activation(T.za[:, E:E + 1], T.c1[:], F.Copy, bias=256.0 - sh, scale=-1.0), "sk2")
-    inc(S.activation(T.pa[:, E + 1:E + 2], T.c1[:], F.Copy, bias=float(sh)), "sk2")
-    v(V.tensor_scalar(T.base[:, 8:120], T.nnp[:, 16:128], 2.0, 8.0, A.mult, A.add))
-    v(V.tensor_scalar(T.base[:, 0:8], T.nnp[:, 8:16], 1.0 if r > 0 else 2.0, 8.0, A.mult, A.add))
-    v(V.tensor_scalar(T.base[:, 120:128], T.nnp[:, 128:136], 1.0 if r < N - 1 else 2.0, 8.0, A.mult, A.add))
-    v(V.memset(T.po[:], 0.0))
-    v(V.memset(T.pf[:], 0.0))
-    v(V.memset(T.zf[:], 0.0))
-    if r == 0:
-        v(V.quantize_mx(T.wx[:, 8:136], T.swx[:, 8:136], T.zt[:]))
-        vw()
-    if r == N - 1:
-        v(V.quantize_mx(T.wx[:, 24:152], T.swx[:, 24:152], T.zt[:]))
-        vw()
-    v(V.quantize_mx(T.wx[:, 16:144], T.swx[:, 16:144], T.xs[:]))
-    wait(V, "sz")
-    v(V.quantize_mx(T.wx[:, 160:288], T.swx[:, 160:288], T.ln[:]))
-    v(V.quantize_mx(T.wx[:, 288:416], T.swx[:, 288:416], T.rn[:]))
+        act(T.base[:, 0:8], T.nnp[:, 8:16], "sk", bias=8.0)
+        act(T.za[:, 0:8], T.zt[:, 0:8], "sk")
+    if r < N - 1:
+        act(T.base[:, 120:128], T.nnp[:, 128:136], "sk", bias=8.0)
+    act(T.po[:, lo:hi], T.zt[:, lo:hi], "sk")
+    act(T.cx[:], T.zt[:], "ez")
+    act(T.pp[:, 112:128], T.zt[:, 0:16], "ez")
+    wait(V, "sx")
+    v(V.quantize_mx(T.wx[:, 6 + 10 * x0:6 + 10 * x1], T.swx[:, 6 + 10 * x0:6 + 10 * x1], T.xp[:, x0:x1, :]))
     wait(V, "dw0")
-    inc(V.quantize_mx(T.qw[:, 0:384], T.sw[:, 0:384], T.wt[:, 0:1536]), "ew")
-    vw()
-    wait(V, "ec")
-    wait(V, "sk")
-    wait(V, "eza")
-    wait(V, "sk2")
 
+    def quantize_w(a, b):
+        for c in range(a, b, 512):
+            d = min(b, c + 512)
+            inc(V.quantize_mx(T.qw[:, c:d], T.sw[:, c:d], T.wt[:, 4 * c:4 * d]), "ew")
+
+    quantize_w(0, WQ)
+    wait(V, "gi3")
+    wait(V, "sk")
+    vw()
+
+    S.wait_ge(T.sem.msg, msg)
     if r > 0:
-        S.wait_ge(T.sem.msg, msg)
-        inc(S.activation(T.jr[:, 0:r], T.mg[:, 0:r, 16], F.Copy, accum_out=T.cr[:]), "ecr")
+        act(T.j0[:, 0:r], T.mg[:, 0:r, 16], "ecr", accum_out=T.cr[:, 0:1])
         wait(S, "ecr")
-        inc(S.activation(T.cr2[:], T.cr[:], F.Copy, bias=-256.0), "ecr2")
+        act(T.cr[:, 1:2], T.cr[:, 0:1], "ecr2", bias=-256.0)
     wait(V, "so")
     V.wait_ge(T.sem.msg, msg)
     if r > 0:
@@ -272,102 +353,118 @@ def rank_program(g, core, T, topo):
         inc(V.tensor_tensor(T.po[:, 0:8], T.mg[:, r, 8:16], T.mg[:, r - 1, 25:33], A.mult), "vq")
     if r < N - 1:
         inc(V.tensor_tensor(T.po[:, 120:128], T.mg[:, r, 17:25], T.mg[:, r + 1, 0:8], A.mult), "vq")
+    cs, sems = (T.cA, T.cB), ("va", "vb")
+
+    def sums(h):
+        if r > 0:
+            wait(V, ("ecr", "ecr2")[h])
+        inc(V.tensor_tensor_scan(cs[h][:, 0:E + 2], T.za[:, 0:E + 2], T.pa[:, 0:E + 2],
+                                 T.cr[:, h:h + 1] if r > 0 else -256.0 * h, A.add, A.add), sems[h])
+
     if r > 0:
         wait(V, "vp")
-        wait(V, "ecr")
-    inc(V.tensor_tensor_scan(T.cA[:, 0:E + 2], T.za[:, 0:E + 2], T.pa[:, 0:E + 2], T.cr[:] if r > 0 else 0.0,
-                             A.add, A.add), "va")
+    sums(0)
     wait(V, "vq")
     inc(V.tensor_tensor_scan(T.rr[:], T.base[:], T.po[:], 0.0, A.add, A.add), "err")
-    if r > 0:
-        wait(V, "ecr2")
-    inc(V.tensor_tensor_scan(T.cB[:, 0:E + 2], T.za[:, 0:E + 2], T.pa[:, 0:E + 2], T.cr2[:] if r > 0 else -256.0,
-                             A.add, A.add), "vb")
-    wait(V, "va")
-    inc(V.tensor_scalar(T.thr[:], T.cA[:, E + 1:E + 2], T.cA[:, E - 1:E] if r > 0 else 0.0, None, A.subtract), "eth")
+    sums(1)
     wait(V, "err")
-    wait(V, "vb")
-    v(V.tensor_scalar(T.cm[:], T.rr[:], T.cB[:, E - 1:E] if r > 0 else -256.0, T.cB[:, E + 1:E + 2], A.add, A.is_le))
-    wait(S, "err")
-    wait(S, "eth")
-    inc(S.activation(T.j3[:], T.rr[:], F.Sign, bias=T.thr[:], scale=-1.0, accum_out=T.acl[:]), "sa")
-    wait(S, "sa")
-    inc(S.activation(T.it[:, 0:32], T.mh[:], F.Copy, scale=T.acl[:]), "et")
-    vw()
-    v(V.tensor_tensor_scan(T.cn[:], T.cm[:], T.zt[:, 0:128], -64.0, A.add, A.add))
-    vw()
-    v(V.tensor_scalar(T.it[:, 32:64], T.m1[:], T.cn[:, 127:128], None, A.mult))
-    wait(V, "et")
-    vw()
-    v(V.transpose(T.tt[:], T.it[:]))
-    vw()
-    v(V.tensor_tensor_scan(T.ss[:], T.rs[:], T.tt[:], 0.0, A.mult, A.add))
-    vw()
-    kk = [T.kk[:, 0:1], T.kk[:, 1:2], 352.0]
+    steps = [
+        lambda h: V.tensor_scalar(T.cm[:, h, 0:128], T.rr[:], cs[h][:, E - 1:E] if r > 0 else -256.0 * h,
+                                  cs[h][:, E + 1:E + 2], A.add, A.is_gt),
+        lambda h: V.tensor_tensor_scan(T.cn[:, h, :], T.cm[:, h, :], T.posn[:, 1:161], 157.0, A.mult, A.max),
+        lambda h: V.transpose(T.tt[:, 32 * h:32 * h + 32], T.cn[:, h, 128:160]),
+        lambda h: V.tensor_tensor_scan(T.ss[:, 32 * h:32 * h + 32], T.ct[:], T.tt[:, 32 * h:32 * h + 32], 0.0, A.add, A.max),
+    ]
+    for step in steps:
+        for h in (0, 1):
+            wait(V, sems[h])
+            inc(step(h), sems[h])
+    act(T.k1[:, 3:4], P16, "s", bias=64.0 * r + 4.0, scale=4.0)
+    act(T.k1[:, 5:6], S32, "s", bias=168.0, scale=1.0 / 32)
+    wait(S, "s")
+    act(T.k1[:, 4:5], S32, "s", F.Identity, bias=T.k1[:, 3:4], scale=-1.75)
+    wait(S, "s")
+    act(T.n2[:], T.jj[:, 0:4], "s", F.Identity, bias=T.k1[:, 4:5], scale=32.0)
+
+    def offsets(name, js, k):
+        inc(V.tensor_scalar(T["off" + name][:, k:3 * len(js):3], T.ss[:, 8 * js[0] + 7:8 * js[-1] + 8:8], -1.0,
+                            T.kk[:, k:k + 1], A.mult, A.add), "eo" + name)
+
+    wait(V, "va")
     for k in range(3):
-        inc(V.tensor_scalar(T.off[:, k:24:3], T.ss[:, 7:64:8], 63.0, kk[k], A.min, A.add), "eo")
+        offsets("a", BATCH[0], k)
+    wait(V, "vb")
+    offsets("b", BATCH[1], 0)
     for q in (V, S):
         q.wait_ge(T.sem.halo, halo)
-        wait(q, "eo")
     for b, js in enumerate(BATCH):
         h = "ab"[b]
-        off = T.off[:, 3 * js[0]:3 * js[0] + 3 * len(js)]
-        inc(V.tensor_copy(T["slot" + h][:].bitcast(dt.uint32), T.wx[:].bitcast(dt.uint32).indirect(off)), "ep" + h)
-        inc(S.activation(T["sslot" + h][:], T.swx[:].indirect(off), F.Copy), "es" + h)
+        n = 48 * len(js)
+        off = T["off" + h][:, 0:3 * len(js)]
+        if b:
+            offsets("b", js, 1)
+            offsets("b", js, 2)
+            offsets("o", [OWN], 0)
+        wait(V, "eo" + h)
+        inc(V.tensor_copy(T["slot" + h][:, 0:n].bitcast(dt.uint32), T.wx[:].bitcast(dt.uint32).indirect(off)), "ep" + h)
+        wait(S, "eo" + h)
+        act(T["sslot" + h][:, 0:n], T.swx[:].indirect(off), "es" + h)
         for plane in (0, 1):
             wait(g, ("es" if plane else "ep") + h)
             tr = []
             for i, (d, es) in enumerate(deal(r, b, plane).items()):
+                via = NH and b == 0 and i == 0
                 i = 48 * i
                 if plane:
-                    src, dst = T["sslot" + h][:, i:i + 40], T.sland[:, 48 * r:48 * r + 40]
+                    src, dst = T["sslot" + h][:, i:i + 40], T.shslot[:, 0:40] if via else T.sland[:, 48 * r:48 * r + 40]
                 else:
                     src = T["slot" + h][:, i:i + 40].bitcast(dt.uint8)
-                    dst = T.land[:, 48 * r:48 * r + 40].bitcast(dt.uint8)
-                tr.append(RemoteDMATransfer(dst_ids=[to(d)], dma_engine_mask=mask(es), remote_sem=T.sem.cod,
-                                            src=src, dst=dst))
-            g.remote_dma_fused(tr, local_sem=T.sem.loc)
+                    dst = (T.hslot[:, 0:40] if via else T.land[:, 48 * r:48 * r + 40]).bitcast(dt.uint8)
+                tr.append(RemoteDMATransfer(dst_ids=[toh(0) if via else to(d)], dma_engine_mask=mask(es),
+                                            remote_sem=T.sem["h%d" % plane] if via else T.sem.cod, src=src, dst=dst))
+            remote(tr, sum(len(es) for es in deal(r, b, plane).values()), "loc")
     cod = 0
     for s in others:
         for b in range(len(BATCH)):
             for plane in (0, 1):
                 cod += len(deal(s, b, plane).get(r, []))
 
-    for k in range(3):
-        inc(V.tensor_scalar(T.offo[:, k:k + 1], T.ss[:, 8 * OWN + 7:8 * OWN + 8], 63.0, kk[k], A.min, A.add), "eo2")
-    v(V.tensor_tensor(T.pf[:, 0:56], T.mg[:, 0:N - 1, 17:25], T.mg[:, 1:N, 0:8], A.mult))
-    v(V.tensor_tensor(T.zf[:, 8:64], T.mg[:, 0:N - 1, 25:33], T.mg[:, 1:N, 8:16], A.mult))
-    v(V.tensor_tensor_scan(T.cc[:], T.mg[:, :, 16], T.zt[:, 0:8], 0.0, A.add, A.add))
-    wait(V, "gi3")
-    v(V.tensor_scalar(T.kr[:], T.kr0[:], T.cf[:, 2:3], 0.125, A.add, A.mult))
-    if r > 0:
-        v(V.tensor_scalar(T.n2[:], T.n0[:], T.hs[:], T.cr[:], A.add, A.add))
-    else:
-        v(V.tensor_scalar(T.n2[:], T.n0[:], T.hs[:], None, A.add))
-    vw()
-    v(V.tensor_tensor_scan(T.cs[:], T.zf[:], T.pf[:], T.cr[:] if r > 0 else 0.0, A.add, A.add))
-    wait(V, "eo2")
-    inc(V.tensor_copy(T.land[:, 48 * r:48 * r + 48].bitcast(dt.uint32),
-                      T.wx[:].bitcast(dt.uint32).indirect(T.offo[:, 0:3])), "ep2")
-    wait(S, "eo2")
-    inc(S.activation(T.sland[:, 48 * r:48 * r + 48], T.swx[:].indirect(T.offo[:, 0:3]), F.Copy), "es2")
-    vw()
-    v(V.tensor_tensor(T.aq[:], T.cc[:], T.cs[:, 7:64:8], A.add))
-    v(V.quantize_mx(T.land[:, 384:512], T.sland[:, 384:512], T.zt[:]))
-    v(V.quantize_mx(T.mv[:, 320:448], T.smv[:, 320:448], T.zt[:]))
-    vw()
+    offsets("o", [OWN], 1)
+    offsets("o", [OWN], 2)
+    if msg2:
+        for q in (V, S):
+            q.wait_ge(T.sem.msg2, msg2)
+    wait(S, "ez")
+    wait(S, "so")
+    act(T.cx[:, 0:128:16], T.mg[:, :, 16], "ecx")
+    inc(V.tensor_tensor(T.pp[:, 0:112], T.mg[:, 0:N - 1, 17:33], T.mg[:, 1:N, 0:16], A.mult), "vp")
+    offo = T.offo[:, 0:3]
+    wait(V, "eoo")
+    inc(V.tensor_copy(T.land[:, 48 * r:48 * r + 48].bitcast(dt.uint32), T.wx[:].bitcast(dt.uint32).indirect(offo)), "ep2")
+    wait(V, "vp")
+    wait(V, "ecx")
+    wait(V, "ez")
+    inc(V.tensor_tensor_scan(T.cs[:, 0:120], T.pp[:, 0:120], T.cx[:, 0:120], 0.0, A.add, A.add), "vf")
+    wait(S, "eoo")
+    act(T.sland[:, 48 * r:48 * r + 48], T.swx[:].indirect(offo), "es2")
+    wait(S, "vf")
+    wait(S, "s")
+    wait(S, "gi4")
     for c in range(4):
-        v(V.tensor_scalar(T.cq[:, 8 * c:8 * c + 8], T.aq[:], T.n2[:, c:c + 1], 48.0, A.is_le, A.mult))
-    vw()
-    v(V.tensor_tensor_scan(T.sq[:], T.rs[:, 0:32], T.cq[:], 0.0, A.mult, A.add))
-    vw()
+        act(T.jr[:, 8 * c:8 * c + 7], T.cs[:, 7:112:16], "s", F.Sign, bias=T.n2[:, c:c + 1], scale=-1.0,
+            accum_out=T.sq[:, c:c + 1])
+    act(T.mj[:], T.nn[:], "s", F.Sign, bias=T.cs[:, 119:120], scale=-1.0)
+    wait(S, "s")
+    act(T.s2[:], T.sq[:], "s", F.Identity, bias=T.k1[:, 5:6], scale=24.0)
+    act(T.mk[:], T.mj[:], "emk", F.Relu)
+    wait(S, "s")
     for k in range(5):
-        inc(V.tensor_scalar(T.offr[:, 4 * k:4 * k + 4], T.sq[:, 7:32:8], T.kr[:, k:k + 1], None, A.add), "er")
+        act(T.of[:, 16 - 4 * k:20 - 4 * k], T.s2[:], "er0", bias=8.0 * k)
 
     wait(V, "dw1")
-    inc(V.quantize_mx(T.qw[:, 384:896], T.sw[:, 384:896], T.wt[:, 1536:3584]), "ew")
-    inc(V.quantize_mx(T.qw[:, 896:1280], T.sw[:, 896:1280], T.wt[:, 3584:5120]), "ew")
-    vw()
+    quantize_w(WQ, 1280)
+    wait(V, "er0")
+    inc(V.tensor_copy(T.offr[:], T.of[:]), "er")
 
     for q in (V, S):
         wait(q, "er")
@@ -375,28 +472,27 @@ def rank_program(g, core, T, topo):
         wait(q, "es2")
         q.wait_ge(T.sem.cod, cod)
     wait(P, "ew")
-    for k in range(5):
-        o16, at = T.offr[:, 4 * k:4 * k + 4], 64 * (4 - k)
-        inc(V.tensor_copy(T.mv[:, at:at + 64].bitcast(dt.uint32),
-                          T.land[:].bitcast(dt.uint32).indirect(o16)), "kv%d" % k)
-        inc(S.activation(T.smv[:, at:at + 64], T.sland[:].indirect(o16), F.Copy), "ks%d" % k)
+    wait(P, "dp")
+    for k, l in PICKS:
+        o16, a, b = T.offr[:, 16 - 4 * l:20 - 4 * k], 64 * (4 - l), 64 * (5 - k)
+        inc(V.tensor_copy(T.mv[:, a:b].bitcast(dt.uint32), T.land[:].bitcast(dt.uint32).indirect(o16)), "kv%d" % k)
+        act(T.smv[:, a:b], T.sland[:].indirect(o16), "ks%d" % k)
     for k in range(5):
         at = 64 * (4 - k)
-        wait(P, "kv%d" % k)
-        wait(P, "ks%d" % k)
+        if k in dict(PICKS):
+            wait(P, "kv%d" % k)
+            wait(P, "ks%d" % k)
         for o in (0, 1):
             w0 = 128 * (2 * k + o)
             i = P.matmul_mx(T.ps[:, 512 * o:512 * o + 128], T.qw[:, w0:w0 + 128], T.sw[:, w0:w0 + 128],
                             T.mv[:, at:at + 128], T.smv[:, at:at + 128], k == 0, k == 4)
             if k == 4:
                 inc(i, "py%d" % o)
-    wait(V, "py0")
-    inc(V.tensor_copy(T.yo[:, 0:64], T.ps[:, 0:64]), "yv")
-    wait(Y, "yv")
-    inc(Y.dma_start(T.y[:, 0:64], T.yo[:, 0:64]), "dy", 16)
-    wait(S, "py1")
-    inc(S.activation(T.yo[:, 64:128], T.ps[:, 512:576], F.Copy), "ys")
-    wait(S, "ys")
-    inc(S.dma_start(T.y[:, 64:128], T.yo[:, 64:128]), "dy", 16)
+    wait(V, "emk")
+    for o, q in enumerate((Y, S)):
+        wait(V, "py%d" % o)
+        inc(V.tensor_tensor(T.yo[:, 64 * o:64 * o + 64], T.ps[:, 512 * o:512 * o + 64], T.mk[:], A.mult), "y%d" % o)
+        wait(q, "y%d" % o)
+        inc(q.dma_start(T.y[:, 64 * o:64 * o + 64], T.yo[:, 64 * o:64 * o + 64]), "dy", 16)
     wait(Y, "dy")
-    g.wait_ge(T.sem.loc, (2 * len(BATCH) + len(near)) * len(engs(others[0])))
+    g.wait_ge(T.sem.loc, sent["loc"])

@@ -9,22 +9,23 @@ BIG = 1.5 * 2.0 ** 32
 ST = 40
 W0 = 3584
 WQ = 896
-NH = 1
-BATCH = ((0, 1, 2), (4, 5, 6, 7))
+NH = 2
+BATCH = ((0, 1), (2,), (4, 5), (6, 7))
 OWN = 3
-PICKS = ((0, 0), (1, 2), (3, 4))
+VIA = {(0, 0): 0, (0, 1): 0, (2, 0): 1}
+CALLS = (((0,), 0), ((1,), 0), ((0, 1), 1), ((2,), 0), ((3,), 0), ((2, 3), 1))
+PRE = 5
 UP, DOWN = 7, 177
 SCRATCH = {
-    "hq": ("sbuf", [128, 16], C4), "hp": ("sbuf", [128, 128], U8),
-    "hslot": ("sbuf", [128, 96], C4), "shslot": ("sbuf", [128, 96], U8),
+    "hq": ("sbuf", [128, 16], C4), "hp": ("sbuf", [128, 32], U8),
+    "hslot": ("sbuf", [128, 48], C4), "shslot": ("sbuf", [128, 48], U8),
     "xs": ("sbuf", [128, 512], BF), "us": ("sbuf", [128, 4], BF), "ut": ("sbuf", [128, 512], BF),
     "xp": ("sbuf", [128, 18, 40], BF), "zt": ("sbuf", [128, 128], BF),
     "wt": ("sbuf", [128, 5120], BF),
     "qu": ("sbuf", [128, 128], C4), "su": ("sbuf", [128, 128], U8),
     "qx": ("sbuf", [128, 128], C4), "sx": ("sbuf", [128, 128], U8),
     "wx": ("sbuf", [128, 192], C4), "swx": ("sbuf", [128, 192], U8),
-    "slota": ("sbuf", [128, 192], C4), "sslota": ("sbuf", [128, 192], U8),
-    "slotb": ("sbuf", [128, 192], C4), "sslotb": ("sbuf", [128, 192], U8),
+    "slot": ("sbuf", [128, 384], C4), "sslot": ("sbuf", [128, 384], U8),
     "land": ("sbuf", [128, 384], C4), "sland": ("sbuf", [128, 384], U8),
     "mv": ("sbuf", [128, 384], C4), "smv": ("sbuf", [128, 384], U8),
     "qw": ("sbuf", [128, 1280], C4), "sw": ("sbuf", [128, 1280], U8),
@@ -32,27 +33,29 @@ SCRATCH = {
     "a4": ("sbuf", [128, 640], BF), "nnp": ("sbuf", [128, 144], BF),
     "mo": ("sbuf", [128, ST * 128], BF), "mg": ("sbuf", [128, 8, 40], BF),
     "base": ("sbuf", [128, 128], BF), "po": ("sbuf", [128, 128], BF),
-    "pa": ("sbuf", [128, 64], BF), "za": ("sbuf", [128, 64], BF), "cr": ("sbuf", [128, 2], F32),
+    "pa": ("sbuf", [128, 64], BF), "za": ("sbuf", [128, 64], BF), "cr": ("sbuf", [128, 1], F32),
     "pp": ("sbuf", [128, 128], BF), "cx": ("sbuf", [128, 128], BF), "cs": ("sbuf", [128, 128], F32),
-    "cA": ("sbuf", [128, 64], F32), "cB": ("sbuf", [128, 64], F32), "rr": ("sbuf", [128, 128], BF),
+    "ca": ("sbuf", [128, 5, 64], F32), "rr": ("sbuf", [128, 128], BF),
     "pi": ("sbuf", [128, 3], "int32"), "ci": ("sbuf", [128, 3], "int32"), "cf": ("sbuf", [128, 3], F32),
     "jj": ("sbuf", [128, 32], F32), "c0": ("sbuf", [128, 32], F32), "ct": ("sbuf", [128, 32], F32),
-    "posn": ("sbuf", [128, 162], BF), "k1": ("sbuf", [128, 8], F32), "kk": ("sbuf", [128, 3], F32),
-    "cm": ("sbuf", [128, 2, 160], BF), "cn": ("sbuf", [128, 2, 160], BF), "j0": ("sbuf", [128, 8], F32),
-    "tt": ("sbuf", [128, 64], BF), "ss": ("sbuf", [128, 64], F32),
-    "offa": ("sbuf", [128, 12], "uint16"), "offb": ("sbuf", [128, 12], "uint16"), "offo": ("sbuf", [128, 4], "uint16"),
+    "pos": ("sbuf", [128, 128], BF), "posn": ("sbuf", [128, 160], BF), "k1": ("sbuf", [128, 8], F32),
+    "kk": ("sbuf", [128, 4], F32), "hh": ("sbuf", [128, 4], F32), "kr": ("sbuf", [128, 5], F32),
+    "cm": ("sbuf", [128, 5, 160], BF), "cn": ("sbuf", [128, 5, 160], BF), "j0": ("sbuf", [128, 8], F32),
+    "tt": ("sbuf", [128, 32], BF), "ss": ("sbuf", [128, 32], F32),
+    "off": ("sbuf", [128, 24], "uint16"), "offo": ("sbuf", [128, 4], "uint16"),
     "n2": ("sbuf", [128, 4], F32), "jr": ("sbuf", [128, 32], F32), "sq": ("sbuf", [128, 4], F32),
-    "s2": ("sbuf", [128, 4], F32), "of": ("sbuf", [128, 20], F32), "offr": ("sbuf", [128, 20], "uint16"),
+    "offr": ("sbuf", [128, 20], "uint16"),
     "nn": ("sbuf", [128, 64], F32), "mj": ("sbuf", [128, 64], F32), "mk": ("sbuf", [128, 64], F32),
-    "jk": ("sbuf", [128, 800], BF), "jl": ("sbuf", [128, 384], BF),
     "yo": ("sbuf", [128, 128], F32),
     "sc": ("psum", [128, 512], F32), "ps": ("psum", [128, 1024], F32),
 }
-SEMAPHORES = ["v", "msg2", "eoo", "z", "du", "dx", "dw0", "dw1", "dp", "gi", "gi2", "gi3", "gi4", "ect", "eut", "eu", "eq", "pm", "esg",
-              "eow", "s1", "ea", "em", "so", "sx", "ei", "ec", "ec0", "ez", "sk", "s", "ecr", "ecr2", "ecx", "err", "eoa",
-              "eob", "epa", "esa", "epb", "esb", "ep2", "es2", "ew", "er", "er0", "emk", "py0", "py1", "y0", "y1", "dy",
-              "vp", "vq", "va", "vb", "vf", "halo", "msg", "cod", "loc", "lm", "hh", "h0", "h1"
-              ] + ["kv%d" % k for k in range(5)] + ["ks%d" % k for k in range(5)]
+SEMAPHORES = (["v", "z", "du", "dx", "dw0", "dw1", "dp", "gi", "gi2", "gi3", "gi4", "ect", "eut", "eu", "eq", "pm", "esg",
+               "eow", "s1", "ea0", "ea1", "en0", "em", "so", "sx", "ei", "ec", "ec0", "ez", "sk", "s", "ecr", "ecx", "err",
+               "eoo", "ep2", "es2", "ew", "er", "er0", "emk", "py0", "py1", "y0", "y1", "dy", "vp", "vq", "vf",
+               "halo", "cod", "cos", "loc", "lm", "hh", "h0", "h1"]
+              + ["m%d" % q for q in range(8)] + ["l%d" % j for j in range(5)]
+              + [h + "%d" % b for h in ("eo", "pv", "pq") for b in range(len(BATCH))]
+              + [h + "%d" % k for h in ("kv", "ks") for k in range(5)])
 
 
 def mask(es):
@@ -66,31 +69,33 @@ def helpers(c, topo):
 def hand_on(g, core, s, i, T, topo):
     N = len(T.cores)
     near = [d for d in (s - 1, s + 1) if 0 <= d < N]
-    on = topo.engines(T.cores[s], core)
-    off = topo.engines(T.cores[s], T.cores[near[0]])
+    inner = len(topo.engines(T.cores[s], core)) - len(topo.engines(T.cores[s], T.cores[near[0]]))
+    sent = [0]
 
-    def send(items, sem):
-        tr = []
-        for j, (d, src, dst) in enumerate(items):
-            es = topo.engines(core, T.cores[d])
-            n = len(es) // len(items)
-            rid, pnc = topo.addr(T.cores[d], core)
-            tr.append(RemoteDMATransfer(dst_ids=[DstId(rid=rid, pnc=pnc)], dma_engine_mask=mask(es[n * j:n * j + n]),
-                                        remote_sem=sem, src=src, dst=dst))
-        g.remote_dma_fused(tr, local_sem=T.sem.loc)
+    def send(d, src, dst, sem):
+        es = topo.engines(core, T.cores[d])
+        rid, pnc = topo.addr(T.cores[d], core)
+        g.remote_dma(dst, src, sem, T.sem.loc, pnc, rid, mask(es))
+        sent[0] += len(es)
 
-    g.wait_ge(T.sem.hh, len(on) - len(off))
-    items = []
-    for d in near:
-        b, c = (UP, 8) if d > s else (DOWN, 0)
-        items.append((d, T.hq[:, c:c + 8].bitcast(dt.uint8), T.wx[:, b:b + 8].bitcast(dt.uint8)))
-    send(items, T.sem.halo)
-    d = (s + BATCH[0][0] - OWN) % N
-    g.wait_ge(T.sem.h0, len(on) - len(off))
-    send([(d, T.hslot[:, 0:40].bitcast(dt.uint8), T.land[:, 48 * s:48 * s + 40].bitcast(dt.uint8))], T.sem.cod)
-    g.wait_ge(T.sem.h1, len(on) - len(off))
-    send([(d, T.shslot[:, 0:40], T.sland[:, 48 * s:48 * s + 40])], T.sem.cod)
-    g.wait_ge(T.sem.loc, 3 * len(topo.engines(core, T.cores[near[0]])))
+    g.wait_ge(T.sem.hh, inner // NH)
+    d = near[-1]
+    a, b = (24, UP) if d > s else (0, DOWN)
+    if len(near) == 1:
+        send(d, T.hp[:, a + 4 * i:a + 4 * i + 4], T.swx[:, b + 4 * i:b + 4 * i + 4], T.sem.halo)
+    elif i:
+        send(d, T.hp[:, a:a + 8], T.swx[:, b:b + 8], T.sem.halo)
+    else:
+        send(d, T.hq[:, 0:8].bitcast(dt.uint8), T.wx[:, b:b + 8].bitcast(dt.uint8), T.sem.halo)
+    for (j, plane), h in sorted(VIA.items()):
+        if h == i:
+            d = (s + j - OWN) % N
+            g.wait_ge(T.sem["h%d" % plane], inner // len([k for js in BATCH if j in js for k in js if (k, plane) in VIA]))
+            if plane:
+                send(d, T.shslot[:, 0:40], T.sland[:, 48 * s:48 * s + 40], T.sem.cos)
+            else:
+                send(d, T.hslot[:, 0:40].bitcast(dt.uint8), T.land[:, 48 * s:48 * s + 40].bitcast(dt.uint8), T.sem.cod)
+    g.wait_ge(T.sem.loc, sent[0])
 
 
 def rank_program(g, core, T, topo):
@@ -102,12 +107,6 @@ def rank_program(g, core, T, topo):
         return
     N = len(T.cores)
     hs = helpers(core, topo)
-    on = topo.engines(core, hs[0]) if NH else []
-
-    def toh(i):
-        rid, pnc = topo.addr(hs[i], core)
-        return DstId(rid=rid, pnc=pnc)
-
     V, S, Y, P = g.vector, g.scalar, g.sync, g.tensor
     cnt = {}
 
@@ -130,12 +129,9 @@ def rank_program(g, core, T, topo):
     def iota(out, pattern, base, name):
         inc(g.iota(out, pattern, base, 0, allow_small_or_imprecise_dtypes=True), name)
 
-    def to(d):
-        rid, pnc = topo.addr(T.cores[d], core)
+    def to(c):
+        rid, pnc = topo.addr(c, core)
         return DstId(rid=rid, pnc=pnc)
-
-    def engs(d, s=r):
-        return topo.engines(T.cores[s], T.cores[d])
 
     others = [(r + j) % N for j in range(1, N)]
 
@@ -143,25 +139,15 @@ def rank_program(g, core, T, topo):
         return [d for d in (s - 1, s + 1) if 0 <= d < N]
 
     near = nears(r)
-    ne = len(engs(near[0]))
+    outer = topo.engines(core, T.cores[near[0]])
+    inner = [e for e in topo.engines(core, hs[0]) if e not in outer]
+    ne = len(outer)
     sent = {"loc": 0, "lm": 0}
 
-    def remote(tr, es, sem):
-        g.remote_dma_fused(tr, local_sem=T.sem[sem])
-        sent[sem] += es
-
-    def deal(s, b, plane):
-        ds = [(s + j - OWN) % N for j in BATCH[b]]
-        es = engs(ds[0], s)
-        n = len(es) // 4
-        w = [1] * 4 if len(ds) == 4 else [2, 1, 1] if plane else [1, 1, 2]
-        if b == 0 and NH:
-            return {ds[0]: [e for e in on if e not in es], ds[1]: es[:2 * n], ds[2]: es[2 * n:]}
-        out, at = {}, 0
-        for d, k in zip(ds, w):
-            out[d] = es[at:at + n * k]
-            at += n * k
-        return out
+    def remote(items, sem):
+        g.remote_dma_fused([RemoteDMATransfer(dst_ids=[to(c)], dma_engine_mask=mask(es), remote_sem=T.sem[sm], src=src, dst=dst)
+                            for c, es, sm, src, dst in items], local_sem=T.sem[sem])
+        sent[sem] += sum(len(i[1]) for i in items)
 
     inc(S.dma_start(T.us[:], T.u[:, 0:4]), "du", 16)
     inc(Y.dma_start(T.xs[:], T.x[:]), "dx", 16)
@@ -170,12 +156,14 @@ def rank_program(g, core, T, topo):
     for c, k in enumerate((8, 32, 16)):
         inc(g.iota(T.pi[:, c:c + 1], [[1, 1]], 0, k), "gi")
     iota(T.jj[:], [[0, 4], [32, 8]], 0, "gi2")
-    iota(T.posn[:, 0:128], [[-10, 16], [-1, 8]], 157, "gi3")
+    iota(T.pos[:], [[10, 16], [1, 8]], 0, "gi3")
     inc(V.memset(T.zt[:], 0.0), "z")
     v(V.memset(T.sgp[:], 0.0))
     for k in range(4):
         v(V.memset(T.ow[:, k:640:5], 1.0 if k else 0.0))
     v(V.memset(T.nnp[:], 0.0))
+    v(V.memset(T.nb[:, 602:640:5], 0.0))
+    v(V.memset(T.nb[:, 3:40:5], 0.0))
     v(V.memset(T.xp[:, :, 0:4], 0.0))
     v(V.memset(T.xp[:, :, 36:40], 0.0))
     x0, x1 = (0 if r == 0 else 1), (18 if r == N - 1 else 17)
@@ -206,39 +194,25 @@ def rank_program(g, core, T, topo):
     wait(P, "eu")
     wait(P, "eq")
     inc(P.matmul_mx(T.sc[:, 0:128], T.qu[:], T.su[:], T.qx[:], T.sx[:], True, True), "pm")
-    E = 8 * r
+    E = PRE + 8 * r
     act(T.pa[:, E:E + 1], T.zt[:, 0:1], "sk", bias=BIG)
     act(T.za[:, E + 1:E + 2], T.zt[:, 0:1], "sk", bias=-BIG)
     wait(S, "dx")
     act(T.xp[:, 1:17, 4:36], T.xs[:], "sx")
 
-    def send_halo(plane, ds, sem):
-        tr = []
-        for i, d in enumerate(ds):
-            a, b = (120, UP) if d > r else (0, DOWN)
-            es = engs(d)
-            n = len(es) // len(ds)
-            if plane:
-                src, dst = T.sx[:, a:a + 8], T.swx[:, b:b + 8]
-            else:
-                src, dst = T.qx[:, a:a + 8].bitcast(dt.uint8), T.wx[:, b:b + 8].bitcast(dt.uint8)
-            tr.append(RemoteDMATransfer(dst_ids=[to(d)], dma_engine_mask=mask(es[n * i:n * i + n]), remote_sem=T.sem.halo,
-                                        src=src, dst=dst))
-        remote(tr, ne, sem)
-
-    def feed_halo():
-        es = [e for e in on if e not in engs(near[0])]
-        n = len(es) // len(near)
-        tr = []
-        for i, d in enumerate(near):
-            a, c = (120, 8) if d > r else (0, 0)
-            tr.append(RemoteDMATransfer(dst_ids=[toh(0)], dma_engine_mask=mask(es[n * i:n * i + n]), remote_sem=T.sem.hh,
-                                        src=T.qx[:, a:a + 8].bitcast(dt.uint8), dst=T.hq[:, c:c + 8].bitcast(dt.uint8)))
-        remote(tr, len(es), "loc")
-
     wait(g, "eq")
-    send_halo(1, near[:1], "lm")
-    halo = sum(ne + ne // len(nears(d)) for d in near)
+    a, b = (120, UP) if near[0] > r else (0, DOWN)
+    items = [(T.cores[near[0]], outer, "halo", T.qx[:, a:a + 8].bitcast(dt.uint8), T.wx[:, b:b + 8].bitcast(dt.uint8))]
+    n = len(inner) // NH
+    for i in range(NH):
+        if i or len(near) == 1:
+            c = 96 if near[-1] > r else 0
+            src, dst = T.sx[:, c:c + 32], T.hp[:]
+        else:
+            src, dst = T.qx[:, 120:128].bitcast(dt.uint8), T.hq[:, 0:8].bitcast(dt.uint8)
+        items.append((hs[i], inner[n * i:n * i + n], "hh", src, dst))
+    remote(items, "lm")
+    halo = sum(ne * (4 - len(nears(d))) for d in near)
 
     n1 = 120 if 0 < r < N - 1 else 128
     b0 = ST * (n1 - 1)
@@ -256,232 +230,275 @@ def rank_program(g, core, T, topo):
         act(T.mo[:, b0:b0 + 8], T.sgp[:, 1, 1:9], "s1", scale=4.0)
     if r < N - 1:
         act(T.mo[:, b0 + 25:b0 + 33], T.sgp[:, 16, 1:9], "s1", scale=4.0)
+    v(V.tensor_scalar(T.nb[:, 2:600:5], T.sc[:, 8:128], -0.5, 0.5, A.max, A.min))
+    v(V.tensor_scalar(T.nb[:, 43:640:5], T.sc[:, 0:120], -0.5, 0.5, A.max, A.min))
     wait(V, "esg")
-    for k, (a, b) in enumerate(((1, 2), (1, 0), (2, 1), (0, 1))):
-        v(V.tensor_scalar(T.nb[:, k:640:5], T.sgp[:, a:a + 16, b:b + 8], 1.0, None, A.mult))
+    for k, (i, j) in enumerate(((1, 2), (1, 0))):
+        v(V.tensor_scalar(T.nb[:, k:640:5], T.sgp[:, i:i + 16, j:j + 8], 1.0, None, A.mult))
     wait(V, "ect")
     wait(V, "eow")
     vw()
-    inc(V.tensor_tensor_scan(T.a4[:], T.ow[:], T.nb[:], 0.0, A.mult, A.add), "ea")
-    wait(V, "ea")
-    v(V.tensor_scalar(T.nnp[:, 8:136], T.a4[:, 4:640:5], 0.0, -4.0, A.is_ge, A.mult))
+    halves = (0, 1) if r > 0 else (1, 0)
+    for h in halves:
+        inc(V.tensor_tensor_scan(T.a4[:, 320 * h:320 * h + 320], T.ow[:, 320 * h:320 * h + 320],
+                                 T.nb[:, 320 * h:320 * h + 320], 0.0, A.mult, A.add), "ea%d" % h)
+    for h in halves:
+        wait(V, "ea%d" % h)
+        inc(V.tensor_scalar(T.nnp[:, 8 + 64 * h:72 + 64 * h], T.a4[:, 320 * h + 4:320 * h + 320:5], 0.0, -4.0,
+                            A.is_ge, A.mult), "en0" if h == halves[0] else "v")
+
+    def row(h):
+        inc(V.tensor_tensor(T.mo[:, b0 + 8 + 9 * h:b0 + 16 + 9 * h], T.nnp[:, 8 + 120 * h:16 + 120 * h],
+                            T.sgp[:, 1 + 15 * h, 1:9], A.mult), "em")
+
+    wait(V, "en0")
+    row(halves[0])
     wait(V, "s1")
     vw()
     d0, d1 = (8, 0) if r == 0 else (8, 16)
     inc(V.tensor_tensor_scan(T.mo[:, 16:b0 + 17:ST], T.nnp[:, d0:d0 + n1], T.nnp[:, d1:d1 + n1], 1024.0,
                              A.add, A.add), "em")
-    if r > 0:
-        inc(V.tensor_tensor(T.mo[:, b0 + 8:b0 + 16], T.nnp[:, 8:16], T.sgp[:, 1, 1:9], A.mult), "em")
-    if r < N - 1:
-        inc(V.tensor_tensor(T.mo[:, b0 + 17:b0 + 25], T.nnp[:, 128:136], T.sgp[:, 16, 1:9], A.mult), "em")
+    if 0 < r < N - 1:
+        row(1)
     wait(g, "em")
     wait(g, "s1")
-    for ds, sem in ((others, "msg"),):
-        if ds:
-            remote([RemoteDMATransfer(dst_ids=[to(d) for d in ds], dma_engine_mask=mask(engs(ds[0])),
-                                      remote_sem=T.sem[sem], srcs=[out], dsts=[T.mg[:, r, m0:m1] for d in ds])], ne, "lm")
+    ds = others[-1:] + others[:-1]
+    g.remote_dma_fused([RemoteDMATransfer(dst_ids=[to(T.cores[d]) for d in ds], dma_engine_mask=mask(outer),
+                                          remote_sem=T.sem["m%d" % r], srcs=[out],
+                                          dsts=[T.mg[:, r, m0:m1] for d in ds])], local_sem=T.sem.lm)
+    sent["lm"] += ne
+
+    def signs(q, ranks):
+        for s in ranks:
+            q.wait_ge(T.sem["m%d" % s], ne)
+
     wait(V, "gi2")
     wait(V, "ec")
     inc(V.tensor_scalar(T.c0[:], T.jj[:], S32, 8448.0, A.not_equal, A.mult), "ec0")
-    v(V.memset(T.cm[:, :, 128:160], 1.0))
-    v(V.memset(T.posn[:, 128:162], 0.0))
-    if NH:
-        feed_halo()
-    else:
-        send_halo(0, near, "loc")
+    v(V.memset(T.cm[:, 4, 128:160], 0.0))
+    v(V.memset(T.posn[:, 127:128], 157.0 / 4))
+    v(V.memset(T.posn[:, 128:160], 64.0))
+    v(V.memset(T.pa[:, 1:PRE - 1], -64.0))
+    v(V.memset(T.pa[:, PRE - 1:PRE], 0.0))
+    v(V.memset(T.za[:, 0:min(E, PRE + 8)], 0.0))
     Y.wait_ge(T.sem.lm, sent["lm"])
     inc(Y.dma_start(T.wt[:, W0:5120], T.w[:, W0:5120]), "dw1", 16)
     inc(Y.dma_start(T.mv[:, 320:384].bitcast(dt.uint8), T.qx[:, 0:64].bitcast(dt.uint8)), "dp", 16)
     inc(Y.dma_start(T.smv[:, 320:384], T.sx[:, 0:64]), "dp", 16)
     if near[1:]:
-        send_halo(1, near[1:], "loc")
+        remote([(T.cores[near[0]], outer, "halo", T.sx[:, a:a + 8], T.swx[:, b:b + 8])], "loc")
     iota(T.nn[:], [[512, 8], [8, 8]], 64 * r + 4, "gi4")
-    msg = ne * len(others)
-    msg2 = ne * len(others) - msg
 
     sh = 64 * ((r - OWN) % N)
     wait(S, "ec")
-    act(T.k1[:, 0:1], P16, "s", bias=1966.0, scale=-10.0 / 128)
-    act(T.k1[:, 1:2], P16, "s", bias=1976.0, scale=-11.0 / 128)
-    act(T.kk[:, 2:3], S32, "sk", bias=1967.0, scale=-8.0)
-    act(T.za[:, E:E + 1], I8, "sk", bias=252.0 - sh, scale=-1.0)
-    act(T.pa[:, E + 1:E + 2], I8, "sk", bias=4.0 + sh)
+    act(T.k1[:, 0:1], S32, "s", F.Identity, bias=P16, scale=-0.5)
+    act(T.k1[:, 1:2], I8, "s", bias=-64.0, scale=-1.0)
+    act(T.za[:, E:E + 1], S32, "sk", bias=252.0 - sh, scale=-0.25)
+    act(T.pa[:, E + 1:E + 2], S32, "sk", bias=4.0 + sh, scale=0.25)
+    act(T.kk[:, 2:3], S32, "sk", bias=-7150.0, scale=32.0)
     wait(S, "s")
-    act(T.kk[:, 0:1], S32, "sk", F.Identity, bias=T.k1[:, 0:1], scale=-8.0 + 10.0 / 256)
-    act(T.kk[:, 1:2], S32, "sk", F.Identity, bias=T.k1[:, 1:2], scale=-8.0 + 11.0 / 256)
+    act(T.hh[:], T.zt[:, 0:4], "s", F.Identity, bias=T.k1[:, 0:1])
+    act(T.k1[:, 2:3], T.k1[:, 0:1], "s", bias=-7151.0, scale=-10.0 / 128)
+    act(T.k1[:, 3:4], T.k1[:, 0:1], "s", bias=-7141.0, scale=-11.0 / 128)
+    act(T.kk[:, 3:4], T.k1[:, 0:1], "sk", bias=17.0, scale=-10.0 / 128)
+    act(T.pa[:, 0:1], S32, "sk", F.Identity, bias=T.k1[:, 1:2], scale=0.25)
+    wait(S, "gi3")
+    act(T.posn[:, 0:127], T.pos[:, 1:128], "sk", scale=0.25)
     wait(S, "em")
     wait(S, "s1")
     act(T.mg[:, r, m0:m1], out, "so")
-    wait(S, "ec0")
-    act(T.ct[:], T.c0[:], "sk", bias=-8192.0)
+    wait(S, "s")
+    act(T.kk[:, 0:1], S32, "sk", F.Identity, bias=T.k1[:, 2:3], scale=32.0)
+    act(T.kk[:, 1:2], S32, "sk", F.Identity, bias=T.k1[:, 3:4], scale=32.0)
+    act(T.cm[:, 0:4, 128], T.hh[:], "sk", bias=2.5, scale=-1.0 / 512)
+    act(T.cm[:, 0:4, 129], T.hh[:], "sk", bias=-2.25, scale=11.0 / 512)
     lo, hi = (8 if r > 0 else 0), (120 if r < N - 1 else 128)
     act(T.base[:, lo:hi], T.nnp[:, lo + 8:hi + 8], "sk", bias=8.0, scale=2.0)
     if r > 0:
         act(T.base[:, 0:8], T.nnp[:, 8:16], "sk", bias=8.0)
-        act(T.za[:, 0:8], T.zt[:, 0:8], "sk")
     if r < N - 1:
         act(T.base[:, 120:128], T.nnp[:, 128:136], "sk", bias=8.0)
     act(T.po[:, lo:hi], T.zt[:, lo:hi], "sk")
-    act(T.cx[:], T.zt[:], "ez")
-    act(T.pp[:, 112:128], T.zt[:, 0:16], "ez")
+    wait(S, "ec0")
+    act(T.ct[:], T.c0[:], "sk", bias=-8192.0)
+    inc(V.memset(T.cx[:], 0.0), "ez")
+    inc(V.memset(T.pp[:, 112:128], 0.0), "ez")
     wait(V, "sx")
     v(V.quantize_mx(T.wx[:, 6 + 10 * x0:6 + 10 * x1], T.swx[:, 6 + 10 * x0:6 + 10 * x1], T.xp[:, x0:x1, :]))
     wait(V, "dw0")
 
     def quantize_w(a, b):
-        for c in range(a, b, 512):
-            d = min(b, c + 512)
-            inc(V.quantize_mx(T.qw[:, c:d], T.sw[:, c:d], T.wt[:, 4 * c:4 * d]), "ew")
+        inc(V.quantize_mx(T.qw[:, a:b], T.sw[:, a:b], T.wt[:, 4 * a:4 * b]), "ew")
 
-    quantize_w(0, WQ)
-    wait(V, "gi3")
+    quantize_w(0, 512)
+    quantize_w(512, WQ)
     wait(V, "sk")
     vw()
 
-    S.wait_ge(T.sem.msg, msg)
+    signs(S, range(r))
     if r > 0:
-        act(T.j0[:, 0:r], T.mg[:, 0:r, 16], "ecr", accum_out=T.cr[:, 0:1])
-        wait(S, "ecr")
-        act(T.cr[:, 1:2], T.cr[:, 0:1], "ecr2", bias=-256.0)
+        act(T.j0[:, 0:r], T.mg[:, 0:r, 16], "ecr", accum_out=T.cr[:])
+
+    def sums(j):
+        i = PRE - 1 - j
+        inc(V.tensor_tensor_scan(T.ca[:, j, i:E + 2], T.za[:, i:E + 2], T.pa[:, i:E + 2], T.cr[:] if r > 0 else 0.0,
+                                 A.add, A.add), "l%d" % j)
+
+    def passed(j):
+        wait(V, "l%d" % j)
+        inc(V.tensor_scalar(T.cm[:, j, 0:128], T.rr[:], T.ca[:, j, E - 1:E], T.ca[:, j, E + 1:E + 2], A.add, A.is_le), "l%d" % j)
+
+    def place(j):
+        n = 130 if j < 4 else 160
+        wait(V, "l%d" % j)
+        inc(V.tensor_tensor_scan(T.cn[:, j, 0:n], T.cm[:, j, 0:n], T.posn[:, 0:n], 0.0, A.add, A.min), "l%d" % j)
+
+    def offsets(out, j, k, name):
+        for i in range(j, k):
+            wait(V, "l%d" % i)
+        inc(V.tensor_scalar(out, T.cn[:, j:k, 127:130], 4.0, T.kk[:, 3:4], A.mult, A.add), name)
+
+    def borders(a, b):
+        inc(V.tensor_tensor(T.pa[:, PRE + 8 * a:PRE + 8 * b], T.mg[:, a:b, 17:25], T.mg[:, a + 1:b + 1, 0:8], A.mult), "vp")
+        b = min(b, r - 1)
+        if b > a:
+            inc(V.tensor_tensor(T.za[:, PRE + 8 * a + 8:PRE + 8 * b + 8], T.mg[:, a:b, 25:33], T.mg[:, a + 1:b + 1, 8:16],
+                                A.mult), "vp")
+
+    order = (4, 0, 1, 2)
     wait(V, "so")
-    V.wait_ge(T.sem.msg, msg)
-    if r > 0:
-        inc(V.tensor_tensor(T.pa[:, 0:E], T.mg[:, 0:r, 17:25], T.mg[:, 1:r + 1, 0:8], A.mult), "vp")
-    if r > 1:
-        inc(V.tensor_tensor(T.za[:, 8:E], T.mg[:, 0:r - 1, 25:33], T.mg[:, 1:r, 8:16], A.mult), "vp")
+    if r == 0:
+        for j in order:
+            sums(j)
+    last = (r + 2) % N
+    signs(V, [d for d in others if d != last])
     if r > 0:
         inc(V.tensor_tensor(T.po[:, 0:8], T.mg[:, r, 8:16], T.mg[:, r - 1, 25:33], A.mult), "vq")
     if r < N - 1:
         inc(V.tensor_tensor(T.po[:, 120:128], T.mg[:, r, 17:25], T.mg[:, r + 1, 0:8], A.mult), "vq")
-    cs, sems = (T.cA, T.cB), ("va", "vb")
-
-    def sums(h):
-        if r > 0:
-            wait(V, ("ecr", "ecr2")[h])
-        inc(V.tensor_tensor_scan(cs[h][:, 0:E + 2], T.za[:, 0:E + 2], T.pa[:, 0:E + 2],
-                                 T.cr[:, h:h + 1] if r > 0 else -256.0 * h, A.add, A.add), sems[h])
-
     if r > 0:
-        wait(V, "vp")
-    sums(0)
+        borders(last + 1 if last < r else 0, r)
+    if last < r:
+        signs(V, [last])
+        borders(0, last + 1)
     wait(V, "vq")
     inc(V.tensor_tensor_scan(T.rr[:], T.base[:], T.po[:], 0.0, A.add, A.add), "err")
-    sums(1)
+    if r > 0:
+        wait(V, "vp")
+        wait(V, "ecr")
+        for j in order:
+            sums(j)
     wait(V, "err")
-    steps = [
-        lambda h: V.tensor_scalar(T.cm[:, h, 0:128], T.rr[:], cs[h][:, E - 1:E] if r > 0 else -256.0 * h,
-                                  cs[h][:, E + 1:E + 2], A.add, A.is_gt),
-        lambda h: V.tensor_tensor_scan(T.cn[:, h, :], T.cm[:, h, :], T.posn[:, 1:161], 157.0, A.mult, A.max),
-        lambda h: V.transpose(T.tt[:, 32 * h:32 * h + 32], T.cn[:, h, 128:160]),
-        lambda h: V.tensor_tensor_scan(T.ss[:, 32 * h:32 * h + 32], T.ct[:], T.tt[:, 32 * h:32 * h + 32], 0.0, A.add, A.max),
-    ]
-    for step in steps:
-        for h in (0, 1):
-            wait(V, sems[h])
-            inc(step(h), sems[h])
-    act(T.k1[:, 3:4], P16, "s", bias=64.0 * r + 4.0, scale=4.0)
-    act(T.k1[:, 5:6], S32, "s", bias=168.0, scale=1.0 / 32)
-    wait(S, "s")
-    act(T.k1[:, 4:5], S32, "s", F.Identity, bias=T.k1[:, 3:4], scale=-1.75)
-    wait(S, "s")
-    act(T.n2[:], T.jj[:, 0:4], "s", F.Identity, bias=T.k1[:, 4:5], scale=32.0)
-
-    def offsets(name, js, k):
-        inc(V.tensor_scalar(T["off" + name][:, k:3 * len(js):3], T.ss[:, 8 * js[0] + 7:8 * js[-1] + 8:8], -1.0,
-                            T.kk[:, k:k + 1], A.mult, A.add), "eo" + name)
-
-    wait(V, "va")
-    for k in range(3):
-        offsets("a", BATCH[0], k)
-    wait(V, "vb")
-    offsets("b", BATCH[1], 0)
-    for q in (V, S):
-        q.wait_ge(T.sem.halo, halo)
-    for b, js in enumerate(BATCH):
-        h = "ab"[b]
-        n = 48 * len(js)
-        off = T["off" + h][:, 0:3 * len(js)]
-        if b:
-            offsets("b", js, 1)
-            offsets("b", js, 2)
-            offsets("o", [OWN], 0)
-        wait(V, "eo" + h)
-        inc(V.tensor_copy(T["slot" + h][:, 0:n].bitcast(dt.uint32), T.wx[:].bitcast(dt.uint32).indirect(off)), "ep" + h)
-        wait(S, "eo" + h)
-        act(T["sslot" + h][:, 0:n], T.swx[:].indirect(off), "es" + h)
-        for plane in (0, 1):
-            wait(g, ("es" if plane else "ep") + h)
-            tr = []
-            for i, (d, es) in enumerate(deal(r, b, plane).items()):
-                via = NH and b == 0 and i == 0
-                i = 48 * i
-                if plane:
-                    src, dst = T["sslot" + h][:, i:i + 40], T.shslot[:, 0:40] if via else T.sland[:, 48 * r:48 * r + 40]
-                else:
-                    src = T["slot" + h][:, i:i + 40].bitcast(dt.uint8)
-                    dst = (T.hslot[:, 0:40] if via else T.land[:, 48 * r:48 * r + 40]).bitcast(dt.uint8)
-                tr.append(RemoteDMATransfer(dst_ids=[toh(0) if via else to(d)], dma_engine_mask=mask(es),
-                                            remote_sem=T.sem["h%d" % plane] if via else T.sem.cod, src=src, dst=dst))
-            remote(tr, sum(len(es) for es in deal(r, b, plane).values()), "loc")
-    cod = 0
-    for s in others:
-        for b in range(len(BATCH)):
-            for plane in (0, 1):
-                cod += len(deal(s, b, plane).get(r, []))
-
-    offsets("o", [OWN], 1)
-    offsets("o", [OWN], 2)
-    if msg2:
-        for q in (V, S):
-            q.wait_ge(T.sem.msg2, msg2)
+    for step in (passed, place):
+        for j in order:
+            step(j)
+    act(T.k1[:, 4:5], P16, "s", bias=64.0 * r + 4.0, scale=4.0)
+    signs(S, others)
     wait(S, "ez")
     wait(S, "so")
     act(T.cx[:, 0:128:16], T.mg[:, :, 16], "ecx")
+    for k in range(5):
+        act(T.kr[:, k:k + 1], S32, "s", bias=168.0 + 8 * k, scale=1.0 / 32)
+    wait(S, "s")
+    act(T.k1[:, 5:6], S32, "s", F.Identity, bias=T.k1[:, 4:5], scale=-1.75)
+    wait(S, "s")
+    act(T.n2[:], T.jj[:, 0:4], "s", F.Identity, bias=T.k1[:, 5:6], scale=32.0)
+
+    wait(V, "l4")
+    inc(V.transpose(T.tt[:], T.cn[:, 4, 128:160]), "l4")
+    offsets(T.off[:, 0:6], 0, 2, "eo0")
+    offsets(T.off[:, 6:9], 2, 3, "eo1")
+    wait(V, "l4")
+    inc(V.tensor_tensor_scan(T.ss[:], T.ct[:], T.tt[:], 0.0, A.add, A.max), "l4")
+    for q in (V, S):
+        q.wait_ge(T.sem.halo, halo)
+    for b, js in enumerate(BATCH):
+        a0, a1 = 3 * js[0], 3 * js[-1] + 3
+        off, eo = T.off[:, a0:a1], "eo%d" % min(b, 2)
+        if b == 1:
+            wait(V, "l4")
+            for k in range(3):
+                inc(V.tensor_scalar(T.off[:, 12 + k:24:3], T.ss[:, 7:32:8], 4.0, T.kk[:, k:k + 1], A.mult, A.add), "eo2")
+        wait(V, eo)
+        inc(V.tensor_copy(T.slot[:, 16 * a0:16 * a1].bitcast(dt.uint32), T.wx[:].bitcast(dt.uint32).indirect(off)), "pv%d" % b)
+        wait(S, eo)
+        act(T.sslot[:, 16 * a0:16 * a1], T.swx[:].indirect(off), "pq%d" % b)
+    cod = [0, 0]
+    for bs, plane in CALLS:
+        js = [j for b in bs for j in BATCH[b]]
+        if True:
+            for b in bs:
+                wait(g, ("pv%d", "pq%d")[plane] % b)
+            direct = [j for j in js if (j, plane) not in VIA]
+            items = []
+            for j in js:
+                if plane:
+                    src, here, there = T.sslot[:, 48 * j:48 * j + 40], T.shslot[:, 0:40], T.sland[:, 48 * r:48 * r + 40]
+                else:
+                    src, here, there = [t.bitcast(dt.uint8) for t in
+                                        (T.slot[:, 48 * j:48 * j + 40], T.hslot[:, 0:40], T.land[:, 48 * r:48 * r + 40])]
+                if j in direct:
+                    n, i = ne // len(direct), direct.index(j)
+                    items.append((T.cores[(r + j - OWN) % N], outer[n * i:n * i + n], ("cod", "cos")[plane], src, there))
+                else:
+                    via = [i for i in js if i not in direct]
+                    n, i = len(inner) // len(via), via.index(j)
+                    items.append((hs[VIA[j, plane]], inner[n * i:n * i + n], "h%d" % plane, src, here))
+            remote(items, "loc")
+            cod[plane] += ne * (len(js) - len(direct) + min(len(direct), 1))
+
+    signs(V, others)
     inc(V.tensor_tensor(T.pp[:, 0:112], T.mg[:, 0:N - 1, 17:33], T.mg[:, 1:N, 0:16], A.mult), "vp")
-    offo = T.offo[:, 0:3]
-    wait(V, "eoo")
-    inc(V.tensor_copy(T.land[:, 48 * r:48 * r + 48].bitcast(dt.uint32), T.wx[:].bitcast(dt.uint32).indirect(offo)), "ep2")
+    sums(OWN)
+    wait(V, "dw1")
+    quantize_w(WQ, WQ + 128)
     wait(V, "vp")
     wait(V, "ecx")
     wait(V, "ez")
     inc(V.tensor_tensor_scan(T.cs[:, 0:120], T.pp[:, 0:120], T.cx[:, 0:120], 0.0, A.add, A.add), "vf")
-    wait(S, "eoo")
-    act(T.sland[:, 48 * r:48 * r + 48], T.swx[:].indirect(offo), "es2")
+    passed(OWN)
+    quantize_w(WQ + 128, WQ + 256)
+    place(OWN)
+    quantize_w(WQ + 256, WQ + 384)
+    offsets(T.offo[:, 0:3], OWN, OWN + 1, "eoo")
     wait(S, "vf")
     wait(S, "s")
     wait(S, "gi4")
     for c in range(4):
-        act(T.jr[:, 8 * c:8 * c + 7], T.cs[:, 7:112:16], "s", F.Sign, bias=T.n2[:, c:c + 1], scale=-1.0,
+        act(T.jr[:, 8 * c:8 * c + 7], T.cs[:, 7:112:16], "er0", F.Sign, bias=T.n2[:, c:c + 1], scale=-1.0,
             accum_out=T.sq[:, c:c + 1])
     act(T.mj[:], T.nn[:], "s", F.Sign, bias=T.cs[:, 119:120], scale=-1.0)
+    wait(S, "eoo")
+    act(T.sland[:, 48 * r:48 * r + 48], T.swx[:].indirect(T.offo[:, 0:3]), "es2")
     wait(S, "s")
-    act(T.s2[:], T.sq[:], "s", F.Identity, bias=T.k1[:, 5:6], scale=24.0)
     act(T.mk[:], T.mj[:], "emk", F.Relu)
-    wait(S, "s")
-    for k in range(5):
-        act(T.of[:, 16 - 4 * k:20 - 4 * k], T.s2[:], "er0", bias=8.0 * k)
-
-    wait(V, "dw1")
-    quantize_w(WQ, 1280)
     wait(V, "er0")
-    inc(V.tensor_copy(T.offr[:], T.of[:]), "er")
+    for k in range(5):
+        inc(V.tensor_scalar(T.offr[:, 16 - 4 * k:20 - 4 * k], T.sq[:], 24.0, T.kr[:, k:k + 1], A.mult, A.add), "er")
+    wait(V, "eoo")
+    inc(V.tensor_copy(T.land[:, 48 * r:48 * r + 48].bitcast(dt.uint32),
+                      T.wx[:].bitcast(dt.uint32).indirect(T.offo[:, 0:3])), "ep2")
 
     for q in (V, S):
         wait(q, "er")
-        wait(q, "ep2")
         wait(q, "es2")
-        q.wait_ge(T.sem.cod, cod)
+    wait(V, "ep2")
     wait(P, "ew")
     wait(P, "dp")
-    for k, l in PICKS:
-        o16, a, b = T.offr[:, 16 - 4 * l:20 - 4 * k], 64 * (4 - l), 64 * (5 - k)
-        inc(V.tensor_copy(T.mv[:, a:b].bitcast(dt.uint32), T.land[:].bitcast(dt.uint32).indirect(o16)), "kv%d" % k)
-        act(T.smv[:, a:b], T.sland[:].indirect(o16), "ks%d" % k)
+
+    def codes(k, a, b):
+        inc(V.tensor_copy(T.mv[:, 16 * a:16 * b].bitcast(dt.uint32),
+                          T.land[:].bitcast(dt.uint32).indirect(T.offr[:, a:b])), "kv%d" % k)
+
+    V.wait_ge(T.sem.cod, cod[0])
+    S.wait_ge(T.sem.cos, cod[1])
+    for k in range(5):
+        codes(k, 16 - 4 * k, 20 - 4 * k)
+        act(T.smv[:, 256 - 64 * k:320 - 64 * k], T.sland[:].indirect(T.offr[:, 16 - 4 * k:20 - 4 * k]), "ks%d" % k)
     for k in range(5):
         at = 64 * (4 - k)
-        if k in dict(PICKS):
-            wait(P, "kv%d" % k)
-            wait(P, "ks%d" % k)
+        wait(P, "kv%d" % k)
+        wait(P, "ks%d" % k)
         for o in (0, 1):
             w0 = 128 * (2 * k + o)
             i = P.matmul_mx(T.ps[:, 512 * o:512 * o + 128], T.qw[:, w0:w0 + 128], T.sw[:, w0:w0 + 128],

from concourse.bass import DstId, RemoteDMATransfer
from concourse.mybir import dt, AluOpType, AxisListType, ActivationFunctionType

A = AluOpType
F = ActivationFunctionType
C4, U8 = "float8_e4m3fn_x4", "uint8"
BF, F32 = "bfloat16", "float32"
BIG = 1.5 * 2.0 ** 32
ST = 40
W0 = 3584
WQ = 896
NH = 2
BATCH = ((0, 1), (2,), (4, 5), (6, 7))
OWN = 3
VIA = {(0, 0): 0, (0, 1): 0, (2, 0): 1}
CALLS = (((0,), 0), ((1,), 0), ((0, 1), 1), ((2,), 0), ((3,), 0), ((2, 3), 1))
PRE = 5
UP, DOWN = 7, 177
SCRATCH = {
    "hq": ("sbuf", [128, 16], C4), "hp": ("sbuf", [128, 32], U8),
    "hslot": ("sbuf", [128, 48], C4), "shslot": ("sbuf", [128, 48], U8),
    "xs": ("sbuf", [128, 512], BF), "us": ("sbuf", [128, 4], BF), "ut": ("sbuf", [128, 512], BF),
    "xp": ("sbuf", [128, 18, 40], BF), "zt": ("sbuf", [128, 128], BF),
    "wt": ("sbuf", [128, 5120], BF),
    "qu": ("sbuf", [128, 128], C4), "su": ("sbuf", [128, 128], U8),
    "qx": ("sbuf", [128, 128], C4), "sx": ("sbuf", [128, 128], U8),
    "wx": ("sbuf", [128, 192], C4), "swx": ("sbuf", [128, 192], U8),
    "slot": ("sbuf", [128, 384], C4), "sslot": ("sbuf", [128, 384], U8),
    "land": ("sbuf", [128, 384], C4), "sland": ("sbuf", [128, 384], U8),
    "mv": ("sbuf", [128, 384], C4), "smv": ("sbuf", [128, 384], U8),
    "qw": ("sbuf", [128, 1280], C4), "sw": ("sbuf", [128, 1280], U8),
    "sgp": ("sbuf", [128, 18, 10], BF), "nb": ("sbuf", [128, 640], BF), "ow": ("sbuf", [128, 640], BF),
    "a4": ("sbuf", [128, 640], BF), "nnp": ("sbuf", [128, 144], BF),
    "mo": ("sbuf", [128, ST * 128], BF), "mg": ("sbuf", [128, 8, 40], BF),
    "base": ("sbuf", [128, 128], BF), "po": ("sbuf", [128, 128], BF),
    "pa": ("sbuf", [128, 64], BF), "za": ("sbuf", [128, 64], BF), "cr": ("sbuf", [128, 1], F32),
    "pp": ("sbuf", [128, 128], BF), "cx": ("sbuf", [128, 128], BF), "cs": ("sbuf", [128, 128], F32),
    "ca": ("sbuf", [128, 5, 64], F32), "rr": ("sbuf", [128, 128], BF),
    "pi": ("sbuf", [128, 3], "int32"), "ci": ("sbuf", [128, 3], "int32"), "cf": ("sbuf", [128, 3], F32),
    "jj": ("sbuf", [128, 32], F32), "c0": ("sbuf", [128, 32], F32), "ct": ("sbuf", [128, 32], F32),
    "pos": ("sbuf", [128, 128], BF), "posn": ("sbuf", [128, 160], BF), "k1": ("sbuf", [128, 8], F32),
    "kk": ("sbuf", [128, 4], F32), "hh": ("sbuf", [128, 4], F32), "kr": ("sbuf", [128, 5], F32),
    "cm": ("sbuf", [128, 5, 160], BF), "cn": ("sbuf", [128, 5, 160], BF), "j0": ("sbuf", [128, 8], F32),
    "tt": ("sbuf", [128, 32], BF), "ss": ("sbuf", [128, 32], F32),
    "off": ("sbuf", [128, 24], "uint16"), "offo": ("sbuf", [128, 4], "uint16"),
    "n2": ("sbuf", [128, 4], F32), "jr": ("sbuf", [128, 32], F32), "sq": ("sbuf", [128, 4], F32),
    "offr": ("sbuf", [128, 20], "uint16"),
    "nn": ("sbuf", [128, 64], F32), "mj": ("sbuf", [128, 64], F32), "mk": ("sbuf", [128, 64], F32),
    "yo": ("sbuf", [128, 128], F32),
    "sc": ("psum", [128, 512], F32), "ps": ("psum", [128, 1024], F32),
}
SEMAPHORES = (["v", "z", "du", "dx", "dw0", "dw1", "dp", "gi", "gi2", "gi3", "gi4", "ect", "eut", "eu", "eq", "pm", "esg",
               "eow", "s1", "ea0", "ea1", "en0", "em", "so", "sx", "ei", "ec", "ec0", "ez", "sk", "s", "ecr", "ecx", "err",
               "eoo", "ep2", "es2", "ew", "er", "er0", "emk", "py0", "py1", "y0", "y1", "dy", "vp", "vq", "vf",
               "halo", "cod", "cos", "loc", "lm", "hh", "h0", "h1"]
              + ["m%d" % q for q in range(8)] + ["l%d" % j for j in range(5)]
              + [h + "%d" % b for h in ("eo", "pv", "pq") for b in range(len(BATCH))]
              + [h + "%d" % k for h in ("kv", "ks") for k in range(5)])


def mask(es):
    return int(sum(1 << e for e in es))


def helpers(c, topo):
    return [h for h in topo.cores_of(c) if topo.die(h) == topo.die(c) and h != c][:NH]


def hand_on(g, core, s, i, T, topo):
    N = len(T.cores)
    near = [d for d in (s - 1, s + 1) if 0 <= d < N]
    inner = len(topo.engines(T.cores[s], core)) - len(topo.engines(T.cores[s], T.cores[near[0]]))
    sent = [0]

    def send(d, src, dst, sem):
        es = topo.engines(core, T.cores[d])
        rid, pnc = topo.addr(T.cores[d], core)
        g.remote_dma(dst, src, sem, T.sem.loc, pnc, rid, mask(es))
        sent[0] += len(es)

    g.wait_ge(T.sem.hh, inner // NH)
    d = near[-1]
    a, b = (24, UP) if d > s else (0, DOWN)
    if len(near) == 1:
        send(d, T.hp[:, a + 4 * i:a + 4 * i + 4], T.swx[:, b + 4 * i:b + 4 * i + 4], T.sem.halo)
    elif i:
        send(d, T.hp[:, a:a + 8], T.swx[:, b:b + 8], T.sem.halo)
    else:
        send(d, T.hq[:, 0:8].bitcast(dt.uint8), T.wx[:, b:b + 8].bitcast(dt.uint8), T.sem.halo)
    for (j, plane), h in sorted(VIA.items()):
        if h == i:
            d = (s + j - OWN) % N
            g.wait_ge(T.sem["h%d" % plane], inner // len([k for js in BATCH if j in js for k in js if (k, plane) in VIA]))
            if plane:
                send(d, T.shslot[:, 0:40], T.sland[:, 48 * s:48 * s + 40], T.sem.cos)
            else:
                send(d, T.hslot[:, 0:40].bitcast(dt.uint8), T.land[:, 48 * s:48 * s + 40].bitcast(dt.uint8), T.sem.cod)
    g.wait_ge(T.sem.loc, sent[0])


def rank_program(g, core, T, topo):
    r = T.rank_of(core)
    if r is None:
        for s, c in enumerate(T.cores):
            if core in helpers(c, topo):
                hand_on(g, core, s, helpers(c, topo).index(core), T, topo)
        return
    N = len(T.cores)
    hs = helpers(core, topo)
    V, S, Y, P = g.vector, g.scalar, g.sync, g.tensor
    cnt = {}

    def inc(i, name, k=1):
        i.then_inc(T.sem[name], k)
        cnt[name] = cnt.get(name, 0) + k

    def wait(q, name):
        q.wait_ge(T.sem[name], cnt[name])

    def v(i):
        inc(i, "v")

    def vw():
        wait(V, "v")

    def act(out, in_, name, func=F.Copy, **kw):
        inc(S.activation(out, in_, func, **kw), name)

    def iota(out, pattern, base, name):
        inc(g.iota(out, pattern, base, 0, allow_small_or_imprecise_dtypes=True), name)

    def to(c):
        rid, pnc = topo.addr(c, core)
        return DstId(rid=rid, pnc=pnc)

    others = [(r + j) % N for j in range(1, N)]

    def nears(s):
        return [d for d in (s - 1, s + 1) if 0 <= d < N]

    near = nears(r)
    outer = topo.engines(core, T.cores[near[0]])
    inner = [e for e in topo.engines(core, hs[0]) if e not in outer]
    ne = len(outer)
    sent = {"loc": 0, "lm": 0}

    def remote(items, sem):
        g.remote_dma_fused([RemoteDMATransfer(dst_ids=[to(c)], dma_engine_mask=mask(es), remote_sem=T.sem[sm], src=src, dst=dst)
                            for c, es, sm, src, dst in items], local_sem=T.sem[sem])
        sent[sem] += sum(len(i[1]) for i in items)

    inc(S.dma_start(T.us[:], T.u[:, 0:4]), "du", 16)
    inc(Y.dma_start(T.xs[:], T.x[:]), "dx", 16)
    inc(Y.dma_start(T.wt[:, 0:W0], T.w[:, 0:W0]), "dw0", 16)

    for c, k in enumerate((8, 32, 16)):
        inc(g.iota(T.pi[:, c:c + 1], [[1, 1]], 0, k), "gi")
    iota(T.jj[:], [[0, 4], [32, 8]], 0, "gi2")
    iota(T.pos[:], [[10, 16], [1, 8]], 0, "gi3")
    inc(V.memset(T.zt[:], 0.0), "z")
    v(V.memset(T.sgp[:], 0.0))
    for k in range(4):
        v(V.memset(T.ow[:, k:640:5], 1.0 if k else 0.0))
    v(V.memset(T.nnp[:], 0.0))
    v(V.memset(T.nb[:, 602:640:5], 0.0))
    v(V.memset(T.nb[:, 3:40:5], 0.0))
    v(V.memset(T.xp[:, :, 0:4], 0.0))
    v(V.memset(T.xp[:, :, 36:40], 0.0))
    x0, x1 = (0 if r == 0 else 1), (18 if r == N - 1 else 17)
    if r in (0, N - 1):
        v(V.memset(T.xp[:, 0 if r == 0 else 17, 4:36], 0.0))
    wait(V, "gi")
    inc(V.tensor_scalar(T.ci[:], T.pi[:], 248, None, A.bitwise_and), "ei")
    I8, S32, P16 = T.cf[:, 0:1], T.cf[:, 1:2], T.cf[:, 2:3]

    wait(S, "z")
    act(T.nb[:, 4:640:5], T.zt[:], "ect", bias=-1.0)
    wait(S, "ect")
    for a, b, st, k, c in ((9, 39, 5, 6, -0.75), (609, 639, 5, 6, -0.75), (44, 600, 40, 14, -0.75), (79, 600, 40, 14, -0.75),
                           (4, 40, 35, 2, -0.5), (604, 640, 35, 2, -0.5)):
        act(T.nb[:, a:b:st], T.zt[:, 0:k], "ect", bias=c)

    wait(S, "du")
    act(T.ut[:, 3:512:4], T.zt[:], "eut", F.Identity, bias=T.us[:, 3:4])
    wait(V, "z")
    wait(V, "du")
    for t in range(3):
        v(V.tensor_scalar(T.ut[:, t:512:4], T.zt[:], T.us[:, t:t + 1], None, A.add))
    wait(V, "eut")
    vw()
    inc(V.quantize_mx(T.qu[:], T.su[:], T.ut[:]), "eu")
    wait(V, "dx")
    inc(V.quantize_mx(T.qx[:], T.sx[:], T.xs[:]), "eq")
    wait(P, "eu")
    wait(P, "eq")
    inc(P.matmul_mx(T.sc[:, 0:128], T.qu[:], T.su[:], T.qx[:], T.sx[:], True, True), "pm")
    E = PRE + 8 * r
    act(T.pa[:, E:E + 1], T.zt[:, 0:1], "sk", bias=BIG)
    act(T.za[:, E + 1:E + 2], T.zt[:, 0:1], "sk", bias=-BIG)
    wait(S, "dx")
    act(T.xp[:, 1:17, 4:36], T.xs[:], "sx")

    wait(g, "eq")
    a, b = (120, UP) if near[0] > r else (0, DOWN)
    items = [(T.cores[near[0]], outer, "halo", T.qx[:, a:a + 8].bitcast(dt.uint8), T.wx[:, b:b + 8].bitcast(dt.uint8))]
    n = len(inner) // NH
    for i in range(NH):
        if i or len(near) == 1:
            c = 96 if near[-1] > r else 0
            src, dst = T.sx[:, c:c + 32], T.hp[:]
        else:
            src, dst = T.qx[:, 120:128].bitcast(dt.uint8), T.hq[:, 0:8].bitcast(dt.uint8)
        items.append((hs[i], inner[n * i:n * i + n], "hh", src, dst))
    remote(items, "lm")
    halo = sum(ne * (4 - len(nears(d))) for d in near)

    n1 = 120 if 0 < r < N - 1 else 128
    b0 = ST * (n1 - 1)
    m0, m1 = (16 if r == 0 else 0), (17 if r == N - 1 else 33)
    out = T.mo[:, b0 + m0:b0 + m1]

    wait(V, "ei")
    inc(V.tensor_copy(T.cf[:], T.ci[:]), "ec")

    wait(V, "pm")
    inc(V.tensor_scalar(T.sgp[:, 1:17, 1:9], T.sc[:, 0:128], -0.5, 0.5, A.max, A.min), "esg")
    wait(S, "esg")
    act(T.ow[:, 4:640:5], T.sgp[:, 1:17, 1:9], "eow")
    if r > 0:
        act(T.mo[:, b0:b0 + 8], T.sgp[:, 1, 1:9], "s1", scale=4.0)
    if r < N - 1:
        act(T.mo[:, b0 + 25:b0 + 33], T.sgp[:, 16, 1:9], "s1", scale=4.0)
    v(V.tensor_scalar(T.nb[:, 2:600:5], T.sc[:, 8:128], -0.5, 0.5, A.max, A.min))
    v(V.tensor_scalar(T.nb[:, 43:640:5], T.sc[:, 0:120], -0.5, 0.5, A.max, A.min))
    wait(V, "esg")
    for k, (i, j) in enumerate(((1, 2), (1, 0))):
        v(V.tensor_scalar(T.nb[:, k:640:5], T.sgp[:, i:i + 16, j:j + 8], 1.0, None, A.mult))
    wait(V, "ect")
    wait(V, "eow")
    vw()
    halves = (0, 1) if r > 0 else (1, 0)
    for h in halves:
        inc(V.tensor_tensor_scan(T.a4[:, 320 * h:320 * h + 320], T.ow[:, 320 * h:320 * h + 320],
                                 T.nb[:, 320 * h:320 * h + 320], 0.0, A.mult, A.add), "ea%d" % h)
    for h in halves:
        wait(V, "ea%d" % h)
        inc(V.tensor_scalar(T.nnp[:, 8 + 64 * h:72 + 64 * h], T.a4[:, 320 * h + 4:320 * h + 320:5], 0.0, -4.0,
                            A.is_ge, A.mult), "en0" if h == halves[0] else "v")

    def row(h):
        inc(V.tensor_tensor(T.mo[:, b0 + 8 + 9 * h:b0 + 16 + 9 * h], T.nnp[:, 8 + 120 * h:16 + 120 * h],
                            T.sgp[:, 1 + 15 * h, 1:9], A.mult), "em")

    wait(V, "en0")
    row(halves[0])
    wait(V, "s1")
    vw()
    d0, d1 = (8, 0) if r == 0 else (8, 16)
    inc(V.tensor_tensor_scan(T.mo[:, 16:b0 + 17:ST], T.nnp[:, d0:d0 + n1], T.nnp[:, d1:d1 + n1], 1024.0,
                             A.add, A.add), "em")
    if 0 < r < N - 1:
        row(1)
    wait(g, "em")
    wait(g, "s1")
    ds = others[-1:] + others[:-1]
    g.remote_dma_fused([RemoteDMATransfer(dst_ids=[to(T.cores[d]) for d in ds], dma_engine_mask=mask(outer),
                                          remote_sem=T.sem["m%d" % r], srcs=[out],
                                          dsts=[T.mg[:, r, m0:m1] for d in ds])], local_sem=T.sem.lm)
    sent["lm"] += ne

    def signs(q, ranks):
        for s in ranks:
            q.wait_ge(T.sem["m%d" % s], ne)

    wait(V, "gi2")
    wait(V, "ec")
    inc(V.tensor_scalar(T.c0[:], T.jj[:], S32, 8448.0, A.not_equal, A.mult), "ec0")
    v(V.memset(T.cm[:, 4, 128:160], 0.0))
    v(V.memset(T.posn[:, 127:128], 157.0 / 4))
    v(V.memset(T.posn[:, 128:160], 64.0))
    v(V.memset(T.pa[:, 1:PRE - 1], -64.0))
    v(V.memset(T.pa[:, PRE - 1:PRE], 0.0))
    v(V.memset(T.za[:, 0:min(E, PRE + 8)], 0.0))
    Y.wait_ge(T.sem.lm, sent["lm"])
    inc(Y.dma_start(T.wt[:, W0:5120], T.w[:, W0:5120]), "dw1", 16)
    inc(Y.dma_start(T.mv[:, 320:384].bitcast(dt.uint8), T.qx[:, 0:64].bitcast(dt.uint8)), "dp", 16)
    inc(Y.dma_start(T.smv[:, 320:384], T.sx[:, 0:64]), "dp", 16)
    if near[1:]:
        remote([(T.cores[near[0]], outer, "halo", T.sx[:, a:a + 8], T.swx[:, b:b + 8])], "loc")
    iota(T.nn[:], [[512, 8], [8, 8]], 64 * r + 4, "gi4")

    sh = 64 * ((r - OWN) % N)
    wait(S, "ec")
    act(T.k1[:, 0:1], S32, "s", F.Identity, bias=P16, scale=-0.5)
    act(T.k1[:, 1:2], I8, "s", bias=-64.0, scale=-1.0)
    act(T.za[:, E:E + 1], S32, "sk", bias=252.0 - sh, scale=-0.25)
    act(T.pa[:, E + 1:E + 2], S32, "sk", bias=4.0 + sh, scale=0.25)
    act(T.kk[:, 2:3], S32, "sk", bias=-7150.0, scale=32.0)
    wait(S, "s")
    act(T.hh[:], T.zt[:, 0:4], "s", F.Identity, bias=T.k1[:, 0:1])
    act(T.k1[:, 2:3], T.k1[:, 0:1], "s", bias=-7151.0, scale=-10.0 / 128)
    act(T.k1[:, 3:4], T.k1[:, 0:1], "s", bias=-7141.0, scale=-11.0 / 128)
    act(T.kk[:, 3:4], T.k1[:, 0:1], "sk", bias=17.0, scale=-10.0 / 128)
    act(T.pa[:, 0:1], S32, "sk", F.Identity, bias=T.k1[:, 1:2], scale=0.25)
    wait(S, "gi3")
    act(T.posn[:, 0:127], T.pos[:, 1:128], "sk", scale=0.25)
    wait(S, "em")
    wait(S, "s1")
    act(T.mg[:, r, m0:m1], out, "so")
    wait(S, "s")
    act(T.kk[:, 0:1], S32, "sk", F.Identity, bias=T.k1[:, 2:3], scale=32.0)
    act(T.kk[:, 1:2], S32, "sk", F.Identity, bias=T.k1[:, 3:4], scale=32.0)
    act(T.cm[:, 0:4, 128], T.hh[:], "sk", bias=2.5, scale=-1.0 / 512)
    act(T.cm[:, 0:4, 129], T.hh[:], "sk", bias=-2.25, scale=11.0 / 512)
    lo, hi = (8 if r > 0 else 0), (120 if r < N - 1 else 128)
    act(T.base[:, lo:hi], T.nnp[:, lo + 8:hi + 8], "sk", bias=8.0, scale=2.0)
    if r > 0:
        act(T.base[:, 0:8], T.nnp[:, 8:16], "sk", bias=8.0)
    if r < N - 1:
        act(T.base[:, 120:128], T.nnp[:, 128:136], "sk", bias=8.0)
    act(T.po[:, lo:hi], T.zt[:, lo:hi], "sk")
    wait(S, "ec0")
    act(T.ct[:], T.c0[:], "sk", bias=-8192.0)
    inc(V.memset(T.cx[:], 0.0), "ez")
    inc(V.memset(T.pp[:, 112:128], 0.0), "ez")
    wait(V, "sx")
    v(V.quantize_mx(T.wx[:, 6 + 10 * x0:6 + 10 * x1], T.swx[:, 6 + 10 * x0:6 + 10 * x1], T.xp[:, x0:x1, :]))
    wait(V, "dw0")

    def quantize_w(a, b):
        inc(V.quantize_mx(T.qw[:, a:b], T.sw[:, a:b], T.wt[:, 4 * a:4 * b]), "ew")

    quantize_w(0, 512)
    quantize_w(512, WQ)
    wait(V, "sk")
    vw()

    signs(S, range(r))
    if r > 0:
        act(T.j0[:, 0:r], T.mg[:, 0:r, 16], "ecr", accum_out=T.cr[:])

    def sums(j):
        i = PRE - 1 - j
        inc(V.tensor_tensor_scan(T.ca[:, j, i:E + 2], T.za[:, i:E + 2], T.pa[:, i:E + 2], T.cr[:] if r > 0 else 0.0,
                                 A.add, A.add), "l%d" % j)

    def passed(j):
        wait(V, "l%d" % j)
        inc(V.tensor_scalar(T.cm[:, j, 0:128], T.rr[:], T.ca[:, j, E - 1:E], T.ca[:, j, E + 1:E + 2], A.add, A.is_le), "l%d" % j)

    def place(j):
        n = 130 if j < 4 else 160
        wait(V, "l%d" % j)
        inc(V.tensor_tensor_scan(T.cn[:, j, 0:n], T.cm[:, j, 0:n], T.posn[:, 0:n], 0.0, A.add, A.min), "l%d" % j)

    def offsets(out, j, k, name):
        for i in range(j, k):
            wait(V, "l%d" % i)
        inc(V.tensor_scalar(out, T.cn[:, j:k, 127:130], 4.0, T.kk[:, 3:4], A.mult, A.add), name)

    def borders(a, b):
        inc(V.tensor_tensor(T.pa[:, PRE + 8 * a:PRE + 8 * b], T.mg[:, a:b, 17:25], T.mg[:, a + 1:b + 1, 0:8], A.mult), "vp")
        b = min(b, r - 1)
        if b > a:
            inc(V.tensor_tensor(T.za[:, PRE + 8 * a + 8:PRE + 8 * b + 8], T.mg[:, a:b, 25:33], T.mg[:, a + 1:b + 1, 8:16],
                                A.mult), "vp")

    order = (4, 0, 1, 2)
    wait(V, "so")
    if r == 0:
        for j in order:
            sums(j)
    last = (r + 2) % N
    signs(V, [d for d in others if d != last])
    if r > 0:
        inc(V.tensor_tensor(T.po[:, 0:8], T.mg[:, r, 8:16], T.mg[:, r - 1, 25:33], A.mult), "vq")
    if r < N - 1:
        inc(V.tensor_tensor(T.po[:, 120:128], T.mg[:, r, 17:25], T.mg[:, r + 1, 0:8], A.mult), "vq")
    if r > 0:
        borders(last + 1 if last < r else 0, r)
    if last < r:
        signs(V, [last])
        borders(0, last + 1)
    wait(V, "vq")
    inc(V.tensor_tensor_scan(T.rr[:], T.base[:], T.po[:], 0.0, A.add, A.add), "err")
    if r > 0:
        wait(V, "vp")
        wait(V, "ecr")
        for j in order:
            sums(j)
    wait(V, "err")
    for step in (passed, place):
        for j in order:
            step(j)
    act(T.k1[:, 4:5], P16, "s", bias=64.0 * r + 4.0, scale=4.0)
    signs(S, others)
    wait(S, "ez")
    wait(S, "so")
    act(T.cx[:, 0:128:16], T.mg[:, :, 16], "ecx")
    for k in range(5):
        act(T.kr[:, k:k + 1], S32, "s", bias=168.0 + 8 * k, scale=1.0 / 32)
    wait(S, "s")
    act(T.k1[:, 5:6], S32, "s", F.Identity, bias=T.k1[:, 4:5], scale=-1.75)
    wait(S, "s")
    act(T.n2[:], T.jj[:, 0:4], "s", F.Identity, bias=T.k1[:, 5:6], scale=32.0)

    wait(V, "l4")
    inc(V.transpose(T.tt[:], T.cn[:, 4, 128:160]), "l4")
    offsets(T.off[:, 0:6], 0, 2, "eo0")
    offsets(T.off[:, 6:9], 2, 3, "eo1")
    wait(V, "l4")
    inc(V.tensor_tensor_scan(T.ss[:], T.ct[:], T.tt[:], 0.0, A.add, A.max), "l4")
    for q in (V, S):
        q.wait_ge(T.sem.halo, halo)
    for b, js in enumerate(BATCH):
        a0, a1 = 3 * js[0], 3 * js[-1] + 3
        off, eo = T.off[:, a0:a1], "eo%d" % min(b, 2)
        if b == 1:
            wait(V, "l4")
            for k in range(3):
                inc(V.tensor_scalar(T.off[:, 12 + k:24:3], T.ss[:, 7:32:8], 4.0, T.kk[:, k:k + 1], A.mult, A.add), "eo2")
        wait(V, eo)
        inc(V.tensor_copy(T.slot[:, 16 * a0:16 * a1].bitcast(dt.uint32), T.wx[:].bitcast(dt.uint32).indirect(off)), "pv%d" % b)
        wait(S, eo)
        act(T.sslot[:, 16 * a0:16 * a1], T.swx[:].indirect(off), "pq%d" % b)
    cod = [0, 0]
    for bs, plane in CALLS:
        js = [j for b in bs for j in BATCH[b]]
        if True:
            for b in bs:
                wait(g, ("pv%d", "pq%d")[plane] % b)
            direct = [j for j in js if (j, plane) not in VIA]
            items = []
            for j in js:
                if plane:
                    src, here, there = T.sslot[:, 48 * j:48 * j + 40], T.shslot[:, 0:40], T.sland[:, 48 * r:48 * r + 40]
                else:
                    src, here, there = [t.bitcast(dt.uint8) for t in
                                        (T.slot[:, 48 * j:48 * j + 40], T.hslot[:, 0:40], T.land[:, 48 * r:48 * r + 40])]
                if j in direct:
                    n, i = ne // len(direct), direct.index(j)
                    items.append((T.cores[(r + j - OWN) % N], outer[n * i:n * i + n], ("cod", "cos")[plane], src, there))
                else:
                    via = [i for i in js if i not in direct]
                    n, i = len(inner) // len(via), via.index(j)
                    items.append((hs[VIA[j, plane]], inner[n * i:n * i + n], "h%d" % plane, src, here))
            remote(items, "loc")
            cod[plane] += ne * (len(js) - len(direct) + min(len(direct), 1))

    signs(V, others)
    inc(V.tensor_tensor(T.pp[:, 0:112], T.mg[:, 0:N - 1, 17:33], T.mg[:, 1:N, 0:16], A.mult), "vp")
    sums(OWN)
    wait(V, "dw1")
    quantize_w(WQ, WQ + 128)
    wait(V, "vp")
    wait(V, "ecx")
    wait(V, "ez")
    inc(V.tensor_tensor_scan(T.cs[:, 0:120], T.pp[:, 0:120], T.cx[:, 0:120], 0.0, A.add, A.add), "vf")
    passed(OWN)
    quantize_w(WQ + 128, WQ + 256)
    place(OWN)
    quantize_w(WQ + 256, WQ + 384)
    offsets(T.offo[:, 0:3], OWN, OWN + 1, "eoo")
    wait(S, "vf")
    wait(S, "s")
    wait(S, "gi4")
    for c in range(4):
        act(T.jr[:, 8 * c:8 * c + 7], T.cs[:, 7:112:16], "er0", F.Sign, bias=T.n2[:, c:c + 1], scale=-1.0,
            accum_out=T.sq[:, c:c + 1])
    act(T.mj[:], T.nn[:], "s", F.Sign, bias=T.cs[:, 119:120], scale=-1.0)
    wait(S, "eoo")
    act(T.sland[:, 48 * r:48 * r + 48], T.swx[:].indirect(T.offo[:, 0:3]), "es2")
    wait(S, "s")
    act(T.mk[:], T.mj[:], "emk", F.Relu)
    wait(V, "er0")
    for k in range(5):
        inc(V.tensor_scalar(T.offr[:, 16 - 4 * k:20 - 4 * k], T.sq[:], 24.0, T.kr[:, k:k + 1], A.mult, A.add), "er")
    wait(V, "eoo")
    inc(V.tensor_copy(T.land[:, 48 * r:48 * r + 48].bitcast(dt.uint32),
                      T.wx[:].bitcast(dt.uint32).indirect(T.offo[:, 0:3])), "ep2")

    for q in (V, S):
        wait(q, "er")
        wait(q, "es2")
    wait(V, "ep2")
    wait(P, "ew")
    wait(P, "dp")

    def codes(k, a, b):
        inc(V.tensor_copy(T.mv[:, 16 * a:16 * b].bitcast(dt.uint32),
                          T.land[:].bitcast(dt.uint32).indirect(T.offr[:, a:b])), "kv%d" % k)

    V.wait_ge(T.sem.cod, cod[0])
    S.wait_ge(T.sem.cos, cod[1])
    for k in range(5):
        codes(k, 16 - 4 * k, 20 - 4 * k)
        act(T.smv[:, 256 - 64 * k:320 - 64 * k], T.sland[:].indirect(T.offr[:, 16 - 4 * k:20 - 4 * k]), "ks%d" % k)
    for k in range(5):
        at = 64 * (4 - k)
        wait(P, "kv%d" % k)
        wait(P, "ks%d" % k)
        for o in (0, 1):
            w0 = 128 * (2 * k + o)
            i = P.matmul_mx(T.ps[:, 512 * o:512 * o + 128], T.qw[:, w0:w0 + 128], T.sw[:, w0:w0 + 128],
                            T.mv[:, at:at + 128], T.smv[:, at:at + 128], k == 0, k == 4)
            if k == 4:
                inc(i, "py%d" % o)
    wait(V, "emk")
    for o, q in enumerate((Y, S)):
        wait(V, "py%d" % o)
        inc(V.tensor_tensor(T.yo[:, 64 * o:64 * o + 64], T.ps[:, 512 * o:512 * o + 64], T.mk[:], A.mult), "y%d" % o)
        wait(q, "y%d" % o)
        inc(q.dma_start(T.y[:, 64 * o:64 * o + 64], T.yo[:, 64 * o:64 * o + 64]), "dy", 16)
    wait(Y, "dy")
    g.wait_ge(T.sem.loc, sent["loc"])
